import numpy as np, ml_dtypes
CORES = [1,5,17,21,33,37,49,53]
N = 8
BF = ml_dtypes.bfloat16
def gentries(a):
    return np.ascontiguousarray(a.reshape(8, 16, -1).transpose(0, 2, 1)).reshape(8, -1)
def gtable(e):
    e = np.asarray(e); return np.ascontiguousarray(e.reshape(8, -1, 16).transpose(0, 2, 1)).reshape(128, -1).astype(np.int32)
W, LN, RO, BL, LG = 4096, 32, 3, 4, 12
SZ = W // LN
DIST = 1 + (np.arange(LN) // BL) % (N - 1)
ROT = (np.arange(16)[:, None] + np.arange(16)[None, :]) % 16
PAT = 255 * np.array([0, 0, 0, 0, 1, 0, 0, 1, 1, 0, 1, 0, 1, 1, 1, 1])
def parts(rng):
    x = rng.integers(0, 256, (N, 8, 16, W)); L = rng.integers(0, W, (N, 8, LN, 16)); c = rng.integers(0, W, (N, 8, LN))
    s = rng.choice(np.array([1.0, 1.3, 1.6]), (N, 8, LN, 1))
    z = np.minimum(np.maximum(np.rint(127.5 + s * (255 * rng.random((N, 8, LN, 16)) - 127.5)), 0), 255).astype(np.int64)
    return x, L, c, z
def mid(rng, x, z, q):
    a = rng.integers(0, W, 512); b = rng.integers(0, LN, 512)
    zz = np.roll(z[:, :, b, :], 5, axis=3).transpose(0, 1, 3, 2)
    d = np.sort(np.sum(np.abs(x[:, :, :, a] - zz), axis=2), axis=2)
    return np.minimum(np.maximum(np.take_along_axis(d, (q * 512).astype(np.int64)[:, :, None], 2)[:, :, 0], 1275), 2295)
def pack(x, L, c, z, t):
    return {"x": x.reshape(N, 128, W).astype(np.float32).astype(BF), "ls": np.stack([gtable(a) for a in L]), "an": c.astype(np.int32),
            "z": np.ascontiguousarray(z.transpose(0, 1, 3, 2)).reshape(N, 128, LN).astype(np.float32).astype(BF), "th": t.reshape(N, 8, 1).astype(np.int32)}
def setup_inputs(rng):
    x, L, c, z = parts(rng)
    return pack(x, L, c, z, mid(rng, x, z, rng.choice(np.array([0.15, 0.22, 0.3, 0.4]), (N, 8))))
def rough(rng, shape, share):
    e = np.minimum(np.exp2(8.1 * rng.random(shape)).astype(np.int64) - 1, 255)
    return np.where(rng.random(shape) < share, 255 - e, e)
def setup_inputs_spread(rng):
    sh = np.array([0.2, 0.5, 0.8])
    x = rough(rng, (N, 8, 16, W), rng.choice(sh, (N, 8, 1, W))); z = rough(rng, (N, 8, LN, 16), rng.choice(sh, (N, 8, LN, 1)))
    e = np.exp2(LG * rng.random((N, 8, LN, 17))).astype(np.int64) - 1
    e = np.where(rng.random(e.shape) < 0.5, W - 1 - e, e)
    return pack(x, e[..., :16], e[..., 16], z, mid(rng, x, z, 0.05 + 0.9 * rng.random((N, 8))))
def setup_inputs_ends(rng):
    sh = np.array([0.3, 0.5, 0.7])
    x = 255 * (rng.random((N, 8, 16, W)) < rng.choice(sh, (N, 8, 1, W))).astype(np.int64)
    z = 255 * (rng.random((N, 8, LN, 16)) < rng.choice(sh, (N, 8, LN, 1))).astype(np.int64)
    L = (W - 1) * (rng.random((N, 8, LN, 16)) < rng.choice(np.array([0.25, 0.5, 0.75]), (N, 8, LN, 1))).astype(np.int64)
    c = (W - 1) * rng.integers(0, 2, (N, 8, LN))
    t = np.where(rng.random((N, 8)) < 0.5, 1275, 2295); t[:, 2] = 1275; t[:, 5] = 2295
    x[:, 1::2, :, 0] = 255; x[:, 1::2, :, W - 1] = 0
    for l, a, b in ((0, 0, 0), (1, W - 1, 0), (2, 0, 255), (3, W - 1, 255), (LN - 4, 0, 0), (LN - 3, W - 1, 255), (LN - 2, W - 1, 0), (LN - 1, 0, 255)):
        L[:, 1::2, l] = 0; c[:, 1::2, l] = a; z[:, 1::2, l] = b
    return pack(x, L, c, z, t)
def setup_inputs_corners(rng):
    x, L, c, z = parts(rng); t = rng.choice(np.array([1275, 1400, 1600, 1800]), (N, 8))
    cnt = np.minimum(np.array([0, 1, 31, 32, 33, LN - 1, LN, 9]), LN)
    for q in range(N):
        order = np.arange(8) if q == 0 else rng.permutation(8)
        for g in range(8):
            hot = rng.permutation(LN) < cnt[order[g]]
            for l in range(LN):
                m = int(rng.choice(np.array([16, 16, 15, 9, 17]))) if hot[l] else int(rng.choice(np.array([8, 8, 1, 0])))
                col = SZ * l + 8 + int(rng.integers(0, 16)); kk = int(rng.choice(np.array([0, 15, int(rng.integers(0, 16))]))) if m == 16 else 0
                zz = np.full(16, 255) if m == 17 else np.roll(PAT, int(rng.integers(0, 16)))
                x[q, g][:, [col - 6, col + 1, col + 6]] = rng.integers(120, 136, (16, 3))
                x[q, g, :, col] = rng.integers(120, 136, 16) if m == 0 else np.roll(zz, -kk)
                c[q, g, l] = col; z[q, g, l] = zz
                L[q, g, l] = 0 if m in (0, 16, 17) else np.where(rng.permutation(16) < m, 0, 6)
    return pack(x, L, c, z, t)
def setup_inputs_ties(rng):
    x, L, c, z = parts(rng); t = mid(rng, x, z, rng.choice(np.array([0.2, 0.3, 0.4]), (N, 8)))
    t[:, ::2] = rng.integers(1275, 2296, (N, 4)); t[0, 0] = 1275; t[N - 1, 6] = 2295
    s = t[:, ::2, None] + rng.integers(-1, 2, (N, 4, LN)); up = rng.random((N, 4, LN)) < 0.5; m = rng.random((N, 4, LN)) < 0.6
    v = (s // 16)[:, :, None, :] + (np.arange(16)[:, None] < (s % 16)[:, :, None, :])
    v = np.where(up[:, :, None, :], 255 - v, v); col = SZ * np.arange(LN) + rng.integers(0, SZ, (N, 4, LN))
    xe = x[:, ::2]; np.put_along_axis(xe, np.repeat(col[:, :, None, :], 16, axis=2), v, 3)
    L[:, ::2] = np.where(m[..., None], 0, L[:, ::2]); c[:, ::2] = np.where(m, col, c[:, ::2]); z[:, ::2] = np.where(m[..., None], 255 * up[..., None], z[:, ::2])
    L[:, 1] = L[:, 1, :1].copy(); c[:, 1] = c[:, 1, :1].copy(); z[:, 1] = z[:, 1][:, np.arange(LN) % 2]
    L[:, 3] = 0; c[:, 3] = W - 1; c[1::2, 3, LN - 1] = 0
    L[:, 5] = rng.choice(np.array([0, 3, W // 2, W - 1]), (N, LN, 16))
    x[:, 7, :, 1::2] = x[:, 7, :, ::2].copy(); L[:, 7, 1::2] = L[:, 7, ::2].copy(); c[:, 7, 1::2] = c[:, 7, ::2].copy()
    return pack(x, L, c, z, t)
def check_inputs(d):
    bad = []
    for k, lo, hi in (("x", 0, 255), ("ls", 0, W - 1), ("an", 0, W - 1), ("z", 0, 255), ("th", 1275, 2295)):
        v = np.asarray(d[k]).astype(np.float64)
        if not (np.min(v) >= lo and np.max(v) <= hi): bad.append("range of " + k)
        elif np.any(v != np.floor(v)): bad.append("whole numbers in " + k)
    return bad
def reference(x, ls, an, z, th):
    X = x.astype(np.float32).astype(np.int64).reshape(N, 8, 16, W)
    L = np.stack([gentries(a) for a in ls]).astype(np.int64).reshape(N, 8, LN, 16)
    c = an.astype(np.int64)
    Z = z.astype(np.float32).astype(np.int64).reshape(N, 8, 16, LN).transpose(0, 1, 3, 2)
    t = th.astype(np.int64).reshape(N, 8); A = np.zeros((N, 8), np.int64)
    src = ((np.arange(N)[:, None] - DIST[None, :]) % N)[:, None, :]; gg = np.arange(8)[None, :, None]; sl = np.arange(LN)[None, None, :]
    k16 = np.arange(16)
    for rnd in range(RO):
        La = L[:, :, :, ROT]; Li = L[:, :, :, None, :]
        E = (((La * Li) >> 5) + La - Li + c[:, :, :, None, None]) & (W - 1)
        ix = E.reshape(N, 8, LN * 256); D = np.zeros(E.shape, np.int64)
        for f in range(16):
            D = D + np.abs(np.take_along_axis(X[:, :, f], ix, 2).reshape(E.shape) - Z[:, :, :, (f + k16) % 16][..., None])
        C = np.sum(D < (t + (A & 31))[:, :, None, None, None], axis=4)
        kt = np.argmax(C, axis=3); kb = np.argmin(C, axis=3)
        win = np.take_along_axis(E, kt[..., None, None], 3)[:, :, :, 0]
        v = np.take_along_axis(np.take_along_axis(E, kb[..., None, None], 3)[:, :, :, 0], kt[..., None], 3)
        M = np.max(np.take_along_axis(X, np.repeat(win.reshape(N, 8, 1, LN * 16), 16, axis=2), 3).reshape(N, 8, 16, LN, 16), axis=4).transpose(0, 1, 3, 2)
        Y = (M + Z) >> 1
        u = np.sum(Y * (2 * k16 + 1), axis=3) & (W - 1)
        A = np.sum(np.max(C, axis=3) >= 9, axis=2)
        place = SZ * np.arange(LN) + (u & (SZ - 1))
        np.put_along_axis(X, np.repeat(place[:, :, None, :], 16, axis=2), Y.transpose(0, 1, 3, 2), 3)
        c = (((u * u) >> 5) + 37 * u + A[:, :, None]) & (W - 1)
        Z = np.abs(Z - M)
        L = np.where(np.roll(k16 == kb[..., None], 1, axis=0), np.roll(v, 1, axis=0), win)
        L = L[src, gg, sl]; c = c[src, gg, sl]; Z = Z[src, gg, sl]
    return {"yx": X.reshape(N, 128, W).astype(np.float32).astype(BF), "yl": np.stack([gtable(a) for a in L]).astype(np.float32), "ya": c.astype(np.float32),
            "yz": np.ascontiguousarray(Z.transpose(0, 1, 3, 2)).reshape(N, 128, LN).astype(np.float32).astype(BF)}

@@ -1,0 +1,581 @@
+import numpy as np
+from concourse.bass import DstId, RemoteDMATransfer
+from concourse.mybir import AluOpType, AxisListType, ActivationFunctionType
+
+N, W, LN, RO, BL = 8, 4096, 32, 3, 4
+DIST = [1 + (l // BL) % (N - 1) for l in range(LN)]
+HOPS = [DIST[BL * b] for b in range(LN // BL)] + [DIST[LN - 1] + 1]
+NB = 14
+MASK_S = True
+YOFF = 1536.0
+K0 = 32.0 * (32 - 40 * 4096)
+
+SCRATCH = {
+    "at8": ("sbuf", [128, 40], "int32"), "af8": ("sbuf", [128, 40], "float32"),
+    "ci": ("sbuf", [128, 8], "int32"), "cf": ("sbuf", [128, 16], "float32"),
+    "iob": ("sbuf", [128, 144], "bfloat16"), "ia": ("sbuf", [128, 256], "bfloat16"), "ib": ("sbuf", [128, 256], "bfloat16"),
+    "tci": ("sbuf", [128, 16], "int32"), "tcf": ("sbuf", [128, 20], "float32"),
+    "pk": ("sbuf", [128, 2048], "float16"), "swp": ("sbuf", [128, 128], "float16"), "mrg": ("sbuf", [128, 64], "float32"),
+    "bw1": ("sbuf", [128, 144], "bfloat16"), "bw2": ("sbuf", [128, 144], "bfloat16"), "bwn": ("sbuf", [128, 144], "bfloat16"),
+    "bwc": ("sbuf", [128, 144], "bfloat16"), "uw": ("sbuf", [128, 144], "bfloat16"),
+    "gio": ("sbuf", [128, 128], "bfloat16"), "blk": ("sbuf", [128, 128], "bfloat16"), "blk32": ("sbuf", [128, 128], "float32"),
+    "gi2": ("sbuf", [128, 128], "bfloat16"), "blk2": ("sbuf", [128, 128], "bfloat16"),
+    "ublk": ("sbuf", [128, 128], "float16"), "nb": ("sbuf", [128, 128], "bfloat16"), "nbt": ("sbuf", [128, 128], "bfloat16"),
+    "ra": ("sbuf", [128, 256], "float16"), "ri": ("sbuf", [128, 256], "float16"),
+    "rib": ("sbuf", [128, 256], "bfloat16"), "hw": ("sbuf", [128, 256], "bfloat16"), "rst": ("sbuf", [128, 256], "bfloat16"),
+    "bdo": ("sbuf", [128, 8], "uint16"), "lof": ("sbuf", [128, 2], "uint16"), "diag": ("sbuf", [128, 16], "float32"),
+    "kp": ("sbuf", [128, 32], "float16"), "kp2": ("sbuf", [128, 32], "float32"),
+    "one": ("sbuf", [128, 128], "bfloat16"), "c20": ("sbuf", [128, 256], "bfloat16"),
+    "snd": ("sbuf", [128, 480], "float32"), "rcv": ("sbuf", [128, 480], "float32"),
+}
+for _h in "01":
+    for _n, _s, _d in (("tab", W, "bfloat16"), ("lsb", 32, "int32"), ("zsb", 32, "bfloat16"), ("sel", 128, "float32"),
+                       ("cin", 64, "float32"), ("col", 8, "float32"), ("hot", 2, "bfloat16"), ("yb", 32, "bfloat16"),
+                       ("plu", 2, "uint16"), ("ot", 96, "float32"), ("of", 64, "float32"), ("oz", 32, "bfloat16"),
+                       ("lm", 16, "int32"), ("li", 16, "int32"), ("lc", 16, "float32"), ("zl", 32, "float16"), ("bd", 128, "float16"),
+                       ("las", 256, "float32"), ("w1", 256, "float32"), ("zr", 256, "bfloat16"), ("sm", 256, "float32"),
+                       ("q", 256, "float32"), ("wi", 256, "int32"), ("e0", 256, "int32"), ("eu", 256, "uint16"),
+                       ("gg", 4096, "bfloat16"), ("mx", 4096, "bfloat16"), ("mask", 256, "bfloat16"),
+                       ("si", 200, "int32"), ("offs", 2, "uint16"), ("winu", 16, "uint16"),
+                       ("xh", 256, "bfloat16"), ("ms", 256, "bfloat16"), ("yh", 16, "float16")):
+        SCRATCH[_n + _h] = ("sbuf", [128, _s], _d)
+    for _n in ("pzl", "pd", "pm", "pll"):
+        SCRATCH[_n + _h] = ("psum", [128, 512], "float32")
+
+SEMAPHORES = (["eV", "eS", "eP", "eG", "sent", "d_an", "d_th"]
+              + ["d_%s%d" % (n, h) for n in ("xa", "xb", "la", "lb", "za", "zb", "yx", "yl", "ya", "yz") for h in range(2)]
+              + ["a%d%d" % (r, h) for r in range(RO) for h in range(2)])
+
+A = AluOpType
+F = ActivationFunctionType
+X = AxisListType.X
+CASES = np.array([[1.04, 0.90, 1.20, 1.04], [1.35, 1.00, 1.70, 1.60], [0.52, 0.45, 0.60, 0.52], [10.0, 0.0, 20.0, 0.0], [30.0, 10.0, 60.0, 30.0],
+                  [70.0, 40.0, 100.0, 60.0], [130.0, 80.0, 200.0, 100.0], [2000.0, 1500.0, 2500.0, 2000.0], [4000.0, 2500.0, 6000.0, 5000.0]])
+CV, CI, CP, FV, FS, LAT_SAME, LAT_X, LAT_DMA, LAT_REM = CASES
+PASSES, TRIES, FRESH = 4, 300, 40
+SG, XH_V = 2, False
+CUTS = ((0, 64), (64, 256))
+PLAN = {}
+
+
+def engine_split(topo, src, dsts):
+    off = [j for j, d in enumerate(dsts) if topo.chip(d) != topo.chip(src)]
+    on = [j for j, d in enumerate(dsts) if topo.chip(d) == topo.chip(src)]
+    out, used = {}, []
+    for part in (off, on):
+        if not part:
+            continue
+        pool = [e for e in topo.engines(src, dsts[part[0]]) if e not in used and all(e in topo.engines(src, dsts[j]) for j in part)]
+        size = [1] * len(part)
+        grow = True
+        while grow:
+            j = size.index(min(size))
+            grow = sum(size) + size[j] <= len(pool)
+            if grow:
+                size[j] *= 2
+        at = 0
+        for j, s in zip(part, size):
+            out[j] = pool[at:at + s]
+            at += s
+        used = used + pool
+    return out
+
+
+def build(T, topo, rank):
+    ops, res, banks, groups, sent = [], {}, {}, [], [0]
+
+    def op(eng, fn, r, w, cost, bank=None, sem=None, acc=None, lat=0.0):
+        k = len(ops)
+        deps = set()
+        for x in r:
+            s = res.setdefault(x, [[], []])
+            deps.update(s[0])
+            s[1].append(k)
+        for x in w:
+            s = res.setdefault(x, [[], []])
+            deps.update(s[0])
+            deps.update(s[1])
+            res[x] = [[k], []]
+        if acc is not None:
+            s = res[acc]
+            deps.add(s[0][0])
+            s[0].append(k)
+        if bank is not None:
+            b = banks.setdefault(bank, [None, [], []])
+            if b[0] != eng:
+                b[0], b[2], b[1] = eng, b[1], []
+            deps.update(b[2])
+            b[1].append(k)
+        deps.discard(k)
+        ops.append({"eng": eng, "fn": fn, "deps": deps, "cost": cost, "sem": sem, "lat": lat})
+        return k
+
+    def n_of(ap):
+        n = 1
+        for s in ap.shape[1:]:
+            n *= s
+        return n
+
+    def ts(out, in0, s1, s2, o0, o1, r, w, bank=None, half=False):
+        c = max(64, n_of(out) * (0.5 if half else 1)) * CV + FV
+        if o1 is None:
+            return op("V", lambda e: e.tensor_scalar(out, in0, s1, None, o0), r, w, c, bank)
+        return op("V", lambda e: e.tensor_scalar(out, in0, s1, s2, o0, o1), r, w, c, bank)
+
+    def tt(out, a, b, o, r, w, bank=None, ind=False):
+        n = n_of(out)
+        c = 50 + n * CI if ind else max(64, n * (1 if bank else 2)) * CV + FV
+        return op("V", lambda e: e.tensor_tensor(out, a, b, o), r, w, c, bank)
+
+    def cp(out, a, r, w, bank=None, c=None):
+        return op("V", lambda e: e.tensor_copy(out, a), r, w, c or max(64, n_of(out)) * CV + FV, bank)
+
+    def red(out, a, o, r, w, bank=None, neg=False):
+        return op("V", lambda e: e.tensor_reduce(out, a, X, o, negate=neg), r, w, 64 * CV + FV, bank)
+
+    def act(out, a, f, r, w, bias=0.0, scale=1.0, bank=None, ind=False, accum=None):
+        n = n_of(out)
+        c = 65 + n * CI if ind else max(64, n) * CV + FS
+        if accum is not None:
+            return op("S", lambda e: e.activation(out, a, f, bias, scale, accum_out=accum), r, w, c + 20, bank)
+        return op("S", lambda e: e.activation(out, a, f, bias, scale), r, w, c, bank)
+
+    def fill(ap, v, w):
+        return iota(ap, [[0, n_of(ap)]], int(v), 0, w)
+
+    def mm(out, lt, rh, r, key, bank, first, f32=False):
+        c = max(64, n_of(out)) * CP * (4 if f32 else 1)
+        fn = lambda e, stop: e.matmul(out, lt, rh, first, stop)
+        if first:
+            k = op("P", fn, r, [key], c, bank)
+            groups.append([k])
+            res[key].append(len(groups) - 1)
+        else:
+            k = op("P", fn, r, [], c, bank, acc=key)
+            groups[res[key][2]].append(k)
+        return k
+
+    def iota(out, pat, base, cm, w, whole=False):
+        if whole:
+            return op("G", lambda e: e.iota(out, pat, base, cm), [], w, 130 + 2 * CV * n_of(out))
+        return op("G", lambda e: e.iota(out, pat, base, cm, allow_small_or_imprecise_dtypes=True), [], w, 130 + 2 * CV * n_of(out))
+
+    def dma(q, out, a, r, w, sem, lat):
+        return op(q, lambda e: e.dma_start(out, a), r, w, 100.0, sem=(sem, 16), lat=lat)
+
+    def exchange(r, h, reads):
+        b, name, me = 80 * (2 * r + h), "a%d%d" % (r, h), T.cores[rank]
+        dst = [T.cores[(rank + d) % N] for d in HOPS]
+        sp = engine_split(topo, me, dst)
+        trs, got = [], 0
+        for j, d in enumerate(dst):
+            rid, pid, _ = topo.addr(d)
+            trs.append(RemoteDMATransfer(dst_ids=[DstId(rid=rid, pnc=pid)], dma_engine_mask=sum(1 << e for e in sp[j]), remote_sem=T.sem[name],
+                                         src=T.snd[:, b + 8 * j:b + 8 * j + 8], dst=T.rcv[:, b + 8 * j:b + 8 * j + 8]))
+            sent[0] += len(sp[j])
+            s = (rank - HOPS[j]) % N
+            got += len(engine_split(topo, T.cores[s], [T.cores[(s + e) % N] for e in HOPS])[j])
+        op("G", lambda e: e.remote_dma_fused(trs, local_sem=T.sem.sent), reads, ["rcv%d%d" % (r, h)], 1000.0, sem=(name, got), lat=LAT_REM)
+
+    dma("S", T.at8[0:8, 0:32], T.an[:], [], ["an"], "d_an", LAT_DMA)
+    dma("S", T.at8[0:8, 32:33], T.th[:], [], ["th"], "d_th", LAT_DMA)
+    prev = None
+    for h in range(2):
+        s = str(h)
+        for n, src, buf, q, lat in (("l", T.ls, "lsb", "Y", LAT_DMA), ("z", T.z, "zsb", "S", LAT_DMA), ("x", T.x, "tab", "Y", LAT_DMA + 3500 * (h + 1))):
+            for c in range(2):
+                k = dma(q, T[buf + s][64 * c:64 * c + 64, :], src[64 * h:64 * h + 64, :], [], [buf + s + "ab"[c]], "d_" + n + "ab"[c] + s, lat)
+                if q == "Y":
+                    if prev is not None:
+                        ops[k]["after"] = prev
+                    prev = k
+
+    cf = T.cf
+    gcol, fcol, g4col, c2col, ecol, ocol, mcol = [cf[:, j:j + 1] for j in range(7)]
+    g15, wcol, lane, scol = [cf[:, j:j + 1] for j in range(7, 11)]
+    iota(T.ci[:, 7:8], [[0, 1]], 0, 1, ["p"], True)
+    iota(T.tci[:], [[-1, 16]], 16, 1, ["tci"], True)
+    iota(T.iob[:], [[1, 144]], 0, 0, ["iob"])
+    iota(T.gio[:], [[16, 8], [0, 16]], 0, 0, ["gio"])
+    iota(T.ia[:], [[1, 16], [1, 16]], 0, 0, ["ia"])
+    iota(T.ib[:], [[1, 16], [0, 16]], 0, 0, ["ib"])
+    for h in range(2):
+        iota(T["sel%d" % h][0:8, :], [[0, 2], [1, 4], [0, 16]], 4 * h, -1, ["sel%d" % h])
+    iota(T.rst[:], [[0, 256]], 1, 0, ["rst"])
+    iota(T.gi2[:], [[0, 2], [16, 4], [0, 16]], 0, 0, ["gi2"])
+    p = T.ci[:, 7:8]
+    for j, m in ((0, 0x70), (1, 15), (2, 0x30), (4, 14), (5, 1), (6, 63)):
+        ts(T.ci[:, j:j + 1], p, m, None, A.bitwise_and, None, ["p"], ["p%d" % j])
+    ts(T.ci[:, 3:4], p, 5, 2, A.arith_shift_right, A.bitwise_and, ["p"], ["p3"])
+    cp(cf[:, 0:7], T.ci[:, 0:7], ["p%d" % j for j in range(7)], ["cf"])
+    ts(T.tci[:], T.tci[:], 15, None, A.bitwise_and, None, ["tci"], ["tci"])
+    ts(T.tcf[:, 0:16], T.tci[:], gcol, None, A.add, None, ["tci", "cf"], ["tcf"])
+    for k in range(16):
+        ts(T.pk[:, 128 * k:128 * k + 128], T.iob[:, 0:128], T.tcf[:, k:k + 1], None, A.is_equal, None, ["iob", "tcf"], ["pk%d" % k], half=True)
+    act(g15, gcol, F.Identity, ["cf"], ["g15"], bias=15.0)
+    act(wcol, fcol, F.Identity, ["cf"], ["wcol"], bias=1.0, scale=2.0)
+    act(cf[:, 11:12], ecol, F.Identity, ["cf"], ["l0"], bias=ocol, scale=2.0)
+    act(lane, cf[:, 11:12], F.Identity, ["cf", "l0"], ["lane"], bias=c2col)
+    act(cf[:, 12:13], lane, F.Identity, ["lane"], ["pb0"], scale=128.0)
+    act(cf[:, 14:15], c2col, F.Identity, ["cf"], ["l1"], bias=256.0, scale=-256.0)
+    act(cf[:, 13:14], cf[:, 14:15], F.Identity, ["l1", "pb0"], ["pb1"], bias=cf[:, 12:13])
+    act(cf[:, 15:16], c2col, F.Identity, ["cf"], ["l2"], bias=64.0, scale=-32.0)
+    act(scol, cf[:, 15:16], F.Identity, ["cf", "l2"], ["scol"], bias=mcol)
+    cp(T.lof[:, 0:1], lane, ["lane"], ["lof"])
+    ts(T.swp[:], T.iob[:, 0:128], scol, None, A.is_equal, None, ["iob", "scol"], ["swp"], half=True)
+    ts(T.mrg[:], T.iob[:, 0:64], mcol, None, A.is_equal, None, ["iob", "cf"], ["mrg"])
+    ts(T.blk[:], T.gio[:], gcol, None, A.is_equal, None, ["gio", "cf"], ["blk"], half=True)
+    ts(T.blk2[:], T.gi2[:], g4col, None, A.is_equal, None, ["gi2", "cf"], ["blk2"], half=True)
+    ts(T.bdo[:], T.iob[:, 0:8], 0.0, fcol, A.mult, A.add, ["iob", "cf"], ["bdo"])
+    ts(T.diag[:], T.iob[:, 0:16], fcol, None, A.is_equal, None, ["iob", "cf"], ["diag"])
+    act(T.tcf[:, 16:17], fcol, F.Identity, ["cf"], ["f8"], bias=-8.0, scale=-1.0)
+    act(T.ia[:], T.ia[:], F.Abs, ["ia", "f8"], ["ia"], bias=T.tcf[:, 16:17])
+    ts(T.ra[:], T.ia[:], 8.0, None, A.is_equal, None, ["ia"], ["ra"], half=True)
+    ts(T.ri[:], T.ib[:], fcol, None, A.is_equal, None, ["ib", "cf"], ["ri"], half=True)
+    ts(T.rib[:], T.ib[:], fcol, None, A.is_equal, None, ["ib", "cf"], ["rib"], half=True)
+    act(T.hw[:], T.rib[:], F.Identity, ["rib"], ["hw"], bias=-8192.0, scale=12288.0)
+    op("G", lambda e: e.affine_select(T.rst[:], T.rst[:], [[0, 16], [1, 16]], A.is_gt, 0.0, 0, 0), ["rst"], ["rst"], 170 + 512 * CV)
+    ts(T.bw1[:], T.iob[:], g15, None, A.is_equal, None, ["iob", "g15"], ["bw1"], half=True)
+    act(T.bw2[:], T.bw1[:], F.Identity, ["bw1"], ["bw2"], scale=2.0)
+    act(T.bwn[:], T.bw1[:], F.Identity, ["bw1"], ["bwn"], scale=-1.0)
+    if MASK_S:
+        act(T.bwc[:], T.bw1[:], F.Identity, ["bw1"], ["bwc"], scale=128.0)
+    act(T.uw[:], T.bw1[:], F.Identity, ["bw1", "wcol"], ["uw"], scale=wcol)
+    ts(T.ublk[:], T.blk[:], wcol, None, A.mult, None, ["blk", "wcol"], ["ublk"], half=True)
+    act(T.blk32[:], T.blk[:], F.Identity, ["blk"], ["blk32"])
+    act(T.nbt[:], T.blk[:], F.Identity, ["blk"], ["nbt"], scale=-1.0)
+    op("G", lambda e: e.affine_select(T.nb[:], T.nbt[:], [[0, 8], [-1, 16]], A.is_ge, 0.0, NB - 1, 0), ["nbt"], ["nb"], 170 + 256 * CV)
+    ts(T.kp[:, 0:16], T.iob[:, 0:16], -16.0, 2048.0 if MASK_S else 0.0, A.mult, A.add, ["iob"], ["kp"])
+    ts(T.kp[:, 16:17], T.iob[:, 0:1], 16384.0, None, A.add, None, ["iob"], ["kpe"])
+    fill(T.kp2[:, 0:16], -32.0, ["kp2"])
+    fill(T.kp2[:, 16:17], 480.0, ["kp3"])
+    act(T.one[0:1, :], T.iob[0:1, 0:128], F.Identity, ["iob"], ["one"], bias=1.0, scale=0.0)
+    act(T.c20[0:1, :], T.ib[0:1, :], F.Identity, ["ib"], ["c20"], bias=2080.0, scale=0.0)
+    fill(T.snd[:], 0.0, ["snd"])
+    cp(T.af8[0:8, 0:33], T.at8[0:8, 0:33], ["an", "th"], ["af8"])
+    for h in range(2):
+        s = str(h)
+        sel = T["sel" + s][0:8, :]
+        ts(sel, sel, 0.0, None, A.is_equal, None, ["sel" + s], ["sel" + s])
+        px = T["pm" + s]
+        mm(px[:, 200:233], sel, T.af8[0:8, 0:33], ["sel" + s, "af8"], "pxb" + s, "pm" + s, True, f32=True)
+        act(T["cin" + s][:, 0:32], px[:, 200:232], F.Identity, ["pxb" + s], ["cin" + s], bias=32.0 * (32 - W), scale=32.0, bank="pm" + s)
+        act(T["col" + s][:, 0:1], px[:, 232:233], F.Identity, ["pxb" + s], ["tcol" + s], bias=-0.5, bank="pm" + s)
+        fill(T["ot" + s][:], 0.0, ["ot0" + s, "ot1" + s, "ot2" + s])
+
+    def lists(r, h):
+        b, s = 80 * (2 * r + h), str(h)
+        lm = T["lm" + s]
+        own = [j for j in range(LN // BL) if (DIST[BL * j] + 1) % N == 0]
+        cuts = [0] + [c for j in own for c in (2 * j, 2 * j + 2)] + [16]
+        for j in range(len(cuts) - 1):
+            lo, hi = cuts[j], cuts[j + 1]
+            src = T.snd if j % 2 else T.rcv
+            tt(lm[:, lo:hi], T.rcv[:, b + 4 * lo:b + 4 * hi:4], src[:, b + 11 + 4 * lo:b + 8 + 4 * hi:4], A.max,
+               ["rcv%d%d" % (r, h), "sP%d%d" % (r, h)], ["lm%s_%d" % (s, j)])
+        ts(T["li" + s][:], lm[:], W - 1, None, A.bitwise_and, None, ["lm%s_%d" % (s, j) for j in range(len(cuts) - 1)], ["li" + s])
+
+    def prep(r, h):
+        s = str(h)
+        t = lambda n: T[n + s]
+        sm, li, kl = t("sm"), t("li")[:], "li" + s
+        if r == 0:
+            lof = T.lof[:, 0:1]
+            cp(li, t("lsb")[:, 0:32].indirect(lof), ["lsb%sa" % s, "lsb%sb" % s, "lof"], [kl], c=80.0)
+            z, c32, kz, kc = t("cin")[:, 32:48], t("cin")[:, 48:64], "z0" + s, "c0" + s
+            act(z, t("zsb")[:, 0:32].indirect(lof), F.Identity, ["zsb%sa" % s, "zsb%sb" % s, "lof"], [kz], ind=True)
+            act(c32, t("cin")[:, 0:32].indirect(lof), F.Identity, ["cin" + s, "lof"], [kc], ind=True)
+        else:
+            lists(r - 1, h)
+            b = 80 * (2 * (r - 1) + h)
+            z, c32 = T.rcv[:, b + 1:b + 64:4], T.rcv[:, b + 2:b + 64:4]
+            kz = kc = "rcv%d%d" % (r - 1, h)
+        ts(t("lc")[:], li, -2048.0, None, A.add, None, [kl], ["lc" + s])
+        ts(t("zl")[:, 1:32:2], li, -2048.0, None, A.add, None, [kl], ["zlL" + s])
+        cp(t("zl")[:, 0:32:2], z, [kz], ["zlz" + s])
+        tt(t("bd")[:], t("lc")[:, 0:16].indirect(T.bdo[:, 0:8]), T.blk[:], A.mult, ["lc" + s, "bdo", "blk"], ["bd" + s], ind=True)
+        pll, kb = t("pll"), "pll" + s
+        pli = t("pd")[:, 256:512]
+        mm(pll[:, 0:256], t("bd")[:], T.ra[:], ["bd" + s, "ra"], "pLa" + s, kb, True)
+        mm(pli, T.one[0:1, :], T.c20[0:1, :], ["one", "c20"], "pLi" + s, "pd" + s, True)
+        mm(pli, t("bd")[:], T.ri[:], ["bd" + s, "ri"], "pLi" + s, "pd" + s, False)
+        for k in range(16):
+            mm(t("pzl")[:, 32 * k:32 * k + 32], T.pk[:, 128 * k:128 * k + 128], t("zl")[:], ["pk%d" % k, "zlL" + s, "zlz" + s],
+               "pzl%s_%d" % (s, k), "pzl" + s, True)
+        kzl = ["pzl%s_%d" % (s, k) for k in range(16)]
+        for j, (a, b) in enumerate(CUTS):
+            act(t("las")[:, a:b], pll[:, a:b], F.Identity, ["pLa" + s], ["las%s%d" % (s, j)], bias=2016.0, bank=kb)
+        act(t("zr")[:], t("pzl")[:, 0:512:2], F.Identity, kzl, ["zr" + s], bank="pzl" + s)
+        act(t("w1")[:], t("pzl")[:, 1:512:2], F.Identity, kzl, ["w1" + s], bias=2016.0, bank="pzl" + s)
+        act(sm[:, 0:16], t("lc")[:], F.Identity, ["lc" + s], ["F0" + s], bias=2080.0)
+        act(sm[:, 16:32], t("lc")[:], F.Identity, ["lc" + s], ["F1" + s], bias=2080.0)
+        act(sm[:, 32:48], z, F.Identity, [kz], ["zq" + s], bias=YOFF - 0.25, scale=0.5)
+        ccol = t("col")[:, 1:2]
+        tt(sm[:, 64:80], c32, T.diag[:], A.mult, [kc, "diag"], ["cd" + s])
+        act(sm[:, 80:96], sm[:, 64:80], F.Identity, ["cd" + s], ["ccol" + s], accum=ccol)
+        act(sm[:, 96:112], c32, F.Identity, [kc], ["c20" + s])
+        act(sm[:, 112:128], c32, F.Identity, [kc], ["c21" + s])
+        for j, (a, b) in enumerate(CUTS):
+            tt(t("q")[:, a:b], t("pd")[:, 256 + a:256 + b], t("las")[:, a:b], A.mult, ["pLi" + s, "las%s%d" % (s, j)], ["q%s%d" % (s, j)], bank="pd" + s)
+        for j, (a, b) in enumerate(CUTS):
+            ts(t("wi")[:, a:b], t("q")[:, a:b], ccol, None, A.add, None, ["q%s%d" % (s, j), "ccol" + s], ["wi%s%d" % (s, j)])
+            ts(t("e0")[:, a:b], t("wi")[:, a:b], 5, W - 1, A.arith_shift_right, A.bitwise_and, ["wi%s%d" % (s, j)], ["e0%s%d" % (s, j)])
+            cp(t("eu")[:, a:b], t("e0")[:, a:b], ["e0%s%d" % (s, j)], ["eu%s%d" % (s, j)])
+
+    def gath(r, h):
+        s = str(h)
+        t = lambda n: T[n + s]
+        win, kw = t("tab")[:, 0:W], ["tab%sa" % s, "tab%sb" % s]
+        kzl = ["pzl%s_%d" % (s, k) for k in range(16)]
+        pd = t("pd")[:, 0:256]
+        mm(pd, T.nb[:], t("zr")[:], ["nb", "zr" + s], "pd" + s, "pd" + s, True)
+        ch = lambda n, i, m=1: t(n)[:, 256 * i:256 * (i + m)]
+        sl = lambda n, i: T[n][:, 15 - i:143 - i]
+        piece = lambda i: ["eu%s%d" % (s, j) for j, (a, b) in enumerate(CUTS) if a <= 16 * i < b]
+        i = 0
+        while i < NB:
+            m = min(SG, NB - i)
+            act(ch("gg", i, m), win.indirect(t("eu")[:, 16 * i:16 * (i + m)]), F.Identity,
+                kw + piece(i) + piece(i + m - 1), ["gg%s_%d" % (s, j) for j in range(i, i + m)], ind=True)
+            i += m
+        for i in range(NB, 16):
+            tt(ch("gg", i), win.indirect(t("eu")[:, 16 * i:16 * i + 16]), t("zr")[:], A.subtract,
+               kw + piece(i) + ["zr" + s], ["gg%s_%d" % (s, i)], ind=True)
+            act(ch("mx", i), ch("gg", i), F.Abs, ["gg%s_%d" % (s, i)], ["mx%s_%d" % (s, i)])
+            mm(pd, sl("bw1", i), ch("mx", i), ["bw1", "mx%s_%d" % (s, i)], "pd" + s, "pd" + s, False)
+        for i in range(NB):
+            tt(ch("mx", i), ch("gg", i), t("pzl")[:, 0:512:2], A.max, ["gg%s_%d" % (s, i)] + kzl, ["mx%s_%d" % (s, i)], bank="pzl" + s)
+            mm(pd, sl("bwn", i), ch("gg", i), ["bwn", "gg%s_%d" % (s, i)], "pd" + s, "pd" + s, False)
+            mm(pd, sl("bw2", i), ch("mx", i), ["bw2", "mx%s_%d" % (s, i)], "pd" + s, "pd" + s, False)
+
+    def counts(r, h):
+        s = str(h)
+        t = lambda n: T[n + s]
+        si, sm, pm, col = t("si"), t("sm"), t("pm"), t("col")
+        thr, kt = (col[:, 0:1], "tcol" + s) if r == 0 else (col[:, 2:3], "thr" + s)
+        if MASK_S:
+            act(t("mask")[:], t("pd")[:, 0:256], F.Sign, ["pd" + s, kt], ["mask" + s], bias=thr, scale=-1.0, bank="pd" + s)
+        else:
+            ts(t("mask")[:], t("pd")[:, 0:256], thr, 256.0, A.is_lt, A.mult, ["pd" + s, kt], ["mask" + s], bank="pd" + s)
+        bw = "bwc" if MASK_S else "bw1"
+        mm(pm[:, 0:17], T.pk[:, 0:128], T.kp[:, 0:17], ["pk0", "kp", "kpe"], "pc" + s, "pm" + s, True)
+        for l in range(16):
+            mm(pm[:, 0:16], T[bw][:, 15 - l:143 - l], t("mask")[:, l:256:16], [bw, "mask" + s], "pc" + s, "pm" + s, False)
+        red(si[:, 175:176], pm[:, 0:16], A.max, ["pc" + s], ["n0" + s], bank="pm" + s, neg=True)
+        op("V", lambda e: e.tensor_tensor_scan(si[:, 176:193], T.kp2[:, 0:17], pm[:, 0:17], 65536.0, A.add, A.min),
+           ["pc" + s, "kp2", "kp3"], ["n1" + s], 64 * CV + FV, "pm" + s)
+        ts(si[:, 2:4], si[:, 175:193:17], 255, None, A.bitwise_and, None, ["n0" + s, "n1" + s], ["na" + s])
+        ts(t("offs")[:], si[:, 2:4], fcol, None, A.add, None, ["na" + s, "cf"], ["offs" + s])
+        ts(t("hot")[:, 0:1], si[:, 175:176], -2048.0, None, A.is_lt, None, ["n0" + s], ["hot" + s])
+        pa = pm[:, 64:65]
+        mm(pa, T.blk2[:], t("hot")[:, 0:1], ["blk2", "hot" + s], "pA" + s, "pm" + s, True)
+        if r < RO - 1:
+            ts(col[:, 4:5], pa, 32.0, pa, A.is_lt, A.mult, ["pA" + s], ["am" + s], bank="pm" + s)
+            act(col[:, 2:3], col[:, 4:5], F.Identity, ["am" + s, "tcol" + s], ["thr" + s], bias=col[:, 0:1])
+        ts(col[:, 3:4], pa, 32.0, K0 if r < RO - 1 else 0.0, A.mult, A.add, ["pA" + s], ["a32" + s], bank="pm" + s)
+
+    def best(r, h):
+        s, rh = str(h), "%d%d" % (r, h)
+        t = lambda n: T[n + s]
+        si, sm, pm, col, offs = t("si"), t("sm"), t("pm"), t("col"), t("offs")
+        b = 80 * (2 * r + h)
+        kw = ["tab%sa" % s, "tab%sb" % s]
+        tt(sm[:, 144:176], t("w1")[:, 0:256].indirect(offs[:, 0:2]), sm[:, 0:32], A.mult, ["w1" + s, "offs" + s, "F0" + s, "F1" + s], ["qw" + s], ind=True)
+        tt(si[:, 16:48], sm[:, 144:176], sm[:, 96:128], A.add, ["qw" + s, "c20" + s, "c21" + s], ["ww" + s])
+        ts(si[:, 48:80], si[:, 16:48], 5, W - 1, A.arith_shift_right, A.bitwise_and, ["ww" + s], ["ew" + s])
+        cp(t("winu")[:], si[:, 48:64], ["ew" + s], ["winu" + s])
+        if XH_V:
+            op("V", lambda e: e.tensor_scalar(t("xh")[:], t("tab")[:, 0:W].indirect(t("winu")[:, 0:16]), 0.5, None, A.mult),
+               kw + ["winu" + s], ["xh" + s], 50 + 256 * CI)
+        else:
+            act(t("xh")[:], t("tab")[:, 0:W].indirect(t("winu")[:, 0:16]), F.Identity, kw + ["winu" + s], ["xh" + s], scale=0.5, ind=True)
+        cp(T.snd[:, b:b + 64:4], si[:, 48:64], ["ew" + s, "snd"], ["sL" + rh])
+        tt(sm[:, 176:192], T.rib[:, 0:256].indirect(offs[:, 0:1]), si[:, 64:80], A.mult, ["rib", "offs" + s, "ew" + s], ["tv" + s], ind=True)
+        act(sm[:, 192:224], T.hw[:, 0:256].indirect(offs[:, 0:2]), F.Identity, ["hw", "offs" + s], ["hb" + s], ind=True)
+        mm(pm[:, 96:112], T.blk32[:], sm[:, 176:192], ["blk32", "tv" + s], "pv" + s, "pm" + s, True, f32=True)
+        tt(T.snd[:, b + 11:b + 72:4], pm[:, 96:112], sm[:, 208:224], A.add, ["pv" + s, "hb" + s, "snd"], ["sP" + rh], bank="pm" + s)
+        op("V", lambda e: e.tensor_tensor_scan(t("ms")[:], T.rst[:], t("xh")[:], 0.0, A.mult, A.max), ["rst", "xh" + s], ["ms" + s], 128 * CV + FV)
+        mh = t("ms")[:, 15:256:16]
+        tt(t("yh")[:], mh, sm[:, 32:48], A.add, ["ms" + s, "zq" + s], ["yh" + s])
+        mm(pm[:, 32:48], T.ublk[:], t("yh")[:], ["ublk", "yh" + s], "pu" + s, "pm" + s, True)
+        pd = t("pd")
+        mm(pd[:, 256:272], T.pk[:, 0:128], t("yh")[:], ["pk0", "yh" + s], "py0" + s, "pd" + s, True)
+        mm(pd[:, 272:288], T.swp[:], t("yh")[:], ["swp", "yh" + s], "py1" + s, "pd" + s, True)
+        act(t("yb")[:], pd[:, 256:288], F.Identity, ["py0" + s, "py1" + s], ["yb" + s], bias=-YOFF, bank="pd" + s)
+        tt(sm[:, 224:240], sm[:, 32:48], mh, A.subtract, ["ms" + s, "zq" + s], ["dz" + s])
+        act(T.snd[:, b + 1:b + 64:4], sm[:, 224:240], F.Abs, ["dz" + s, "snd"], ["sZ" + rh], bias=0.5 - 2 * YOFF, scale=2.0)
+        cp(si[:, 80:96], pm[:, 32:48], ["pu" + s], ["ui" + s], bank="pm" + s)
+        ts(si[:, 96:112], si[:, 80:96], W - 1, None, A.bitwise_and, None, ["ui" + s], ["u" + s])
+        tt(si[:, 112:128], si[:, 96:112], si[:, 96:112], A.mult, ["u" + s], ["sq" + s])
+        ts(si[:, 128:144], si[:, 112:128], 32 * W - 32, None, A.bitwise_and, None, ["sq" + s], ["s" + s])
+        ts(sm[:, 240:256], si[:, 96:112], 1184.0, col[:, 3:4], A.mult, A.add, ["u" + s, "a32" + s], ["r" + s])
+        out = T.snd[:, b + 2:b + 64:4]
+        if r < RO - 1:
+            tt(out, si[:, 128:144], sm[:, 240:256], A.add, ["s" + s, "r" + s, "snd"], ["sC" + rh])
+        else:
+            tt(si[:, 144:160], si[:, 128:144], sm[:, 240:256], A.add, ["s" + s, "r" + s], ["c1" + s])
+            ts(si[:, 160:176], si[:, 144:160], 5, W - 1, A.arith_shift_right, A.bitwise_and, ["c1" + s], ["c2" + s])
+            cp(out, si[:, 160:176], ["c2" + s, "snd"], ["sC" + rh])
+        exchange(r, h, ["sL" + rh, "sZ" + rh, "sC" + rh, "sP" + rh])
+        for l in range(16):
+            mm(pd[:, 288:290], T.uw[:, 15 - l:143 - l], t("yb")[:, l:32:16], ["uw", "yb" + s], "pt" + s, "pd" + s, l == 0)
+        cp(si[:, 4:6], pd[:, 288:290], ["pt" + s], ["pli" + s], bank="pd" + s)
+        ts(si[:, 6:8], si[:, 4:6], 127, None, A.bitwise_and, None, ["pli" + s], ["plj" + s])
+        for c in range(2):
+            ts(t("plu")[:, c:c + 1], si[:, 6 + c:7 + c], cf[:, 12 + c:13 + c], None, A.add, None, ["plj" + s, "pb%d" % c], ["plu%d%s" % (c, s)])
+        cp(t("tab")[:, 0:W].indirect(t("plu")[:, 0:2]), t("yb")[:], ["plu0" + s, "plu1" + s, "yb" + s], kw, c=180.0)
+        if r == RO - 1:
+            dma("Y", T.yx[64 * h:64 * h + 64, :], t("tab")[0:64, :], kw, ["yx" + s], "d_yx" + s, LAT_DMA + 1800)
+
+    def leave(h):
+        s, b = str(h), 80 * (2 * (RO - 1) + h)
+        t = lambda n: T[n + s]
+        key, ot, lof, pm = "rcv%d%d" % (RO - 1, h), t("ot"), T.lof[:, 0:1], t("pm")
+        lists(RO - 1, h)
+        cp(ot[:, 32:64].indirect(lof), T.rcv[:, b + 2:b + 64:4], [key, "lof"], ["ot1" + s], c=110.0)
+        cp(ot[:, 64:96].indirect(lof), T.rcv[:, b + 1:b + 64:4], [key, "lof"], ["ot2" + s], c=110.0)
+        cp(ot[:, 0:32].indirect(lof), t("li")[:], ["li" + s, "lof"], ["ot0" + s], c=110.0)
+        mm(pm[0:64, 96:160], T.mrg[:], ot[:, 32:96], ["mrg", "ot1" + s, "ot2" + s], "po1" + s, "pm" + s, True, f32=True)
+        act(t("oz")[0:64, :], pm[0:64, 128:160], F.Identity, ["po1" + s], ["oz" + s], bank="pm" + s)
+        act(t("of")[0:64, 32:64], pm[0:64, 96:128], F.Identity, ["po1" + s], ["oc" + s], bank="pm" + s)
+        pz = t("pzl")
+        mm(pz[0:64, 0:32], T.mrg[:], ot[:, 0:32], ["mrg", "ot0" + s], "pzl%s_0" % s, "pzl" + s, True, f32=True)
+        cp(t("of")[0:64, 0:32], pz[0:64, 0:32], ["pzl%s_0" % s], ["ol" + s], bank="pzl" + s)
+        dma("S", T.yz[64 * h:64 * h + 64, :], t("oz")[0:64, :], ["oz" + s], ["yz" + s], "d_yz" + s, LAT_DMA)
+        dma("S", T.ya[4 * h:4 * h + 4, :], t("of")[0:64:16, 32:64], ["oc" + s], ["ya" + s], "d_ya" + s, LAT_DMA)
+        dma("Y", T.yl[64 * h:64 * h + 64, :], t("of")[0:64, 0:32], ["ol" + s], ["yl" + s], "d_yl" + s, LAT_DMA)
+
+    prep(0, 0)
+    prep(0, 1)
+    for r in range(RO):
+        for h in range(2):
+            gath(r, h)
+            if h == 0 and r > 0:
+                prep(r, 1)
+            counts(r, h)
+            best(r, h)
+            if h == 1 and r < RO - 1:
+                prep(r + 1, 0)
+    leave(0)
+    leave(1)
+    return ops, groups, sent[0]
+
+
+def plan(ops):
+    n = len(ops)
+    nil = 0.0 * CV
+    cases = []
+    for c in range(len(CV)):
+        lat = [float((o["lat"] + nil)[c]) for o in ops]
+        pred = [[(d, lat[d] if ops[d]["sem"] is not None else float(LAT_X[c]) if ops[d]["eng"] != o["eng"]
+                  else 0.0 if o["eng"] == "P" else float(LAT_SAME[c])) for d in sorted(o["deps"])]
+                + ([(o["after"], 0.0)] if "after" in o else []) for o in ops]
+        succ = [[] for _ in ops]
+        for k in range(n):
+            for d, gap in pred[k]:
+                succ[d].append((k, gap))
+        cases.append(([float((o["cost"] + nil)[c]) for o in ops], lat, pred, succ))
+
+    def replay(order, case):
+        cost, lat, pred, _ = case
+        free, st = {e: 0.0 for e in "VSPGY"}, [0.0] * n
+        for k in order:
+            st[k] = max([st[j] + cost[j] + gap for j, gap in pred[k]] + [free[ops[k]["eng"]]])
+            free[ops[k]["eng"]] = st[k] + cost[k]
+        return max(st[k] + cost[k] + lat[k] for k in range(n)), st
+
+    def place(seq, back, cost, slack, case):
+        _, lat, pred, succ = case
+        busy = {e: [] for e in "VSPGY"}
+        st = [0.0] * n
+        for k in seq:
+            c = cost[k]
+            t = max([st[j] + cost[j] + gap * slack for j, gap in (succ[k] if back else pred[k])] + [lat[k] if back else 0.0])
+            line = busy[ops[k]["eng"]]
+            lo, hi = 0, len(line)
+            while lo < hi:
+                m = (lo + hi) // 2
+                if line[m][1] <= t:
+                    lo = m + 1
+                else:
+                    hi = m
+            while lo < len(line) and line[lo][0] < t + c:
+                t = max(t, line[lo][1])
+                lo += 1
+            line.insert(lo, (t, t + c))
+            st[k] = t
+        return st
+
+    best, rng = None, np.random.default_rng(7)
+    for j in range(TRIES):
+        case = cases[j % len(cases)]
+        cost = [c * (0.85 + 0.3 * float(rng.random())) for c in case[0]]
+        slack = 0.8 + 0.8 * float(rng.random())
+        seq = list(range(n)) if j < FRESH else best[1]
+        for _ in range(PASSES):
+            st = place(seq, False, cost, slack, case)
+            order = sorted(range(n), key=lambda k: (st[k], k))
+            ends = [replay(order, c)[0] for c in cases]
+            if best is None or sum(ends) < sum(best[0]):
+                best = (ends, order)
+            bk = place(sorted(range(n), key=lambda k: (-st[k] - cost[k], -k)), True, cost, slack, case)
+            seq = sorted(range(n), key=lambda k: (-bk[k] - cost[k], k))
+    return best[1], replay(best[1], cases[0])[1], best[0], cases[0][0]
+
+
+def rank_program(g, core, T, topo):
+    rank = T.rank_of(core)
+    if rank is None:
+        return
+    ops, groups, sent = build(T, topo, rank)
+    if "order" not in PLAN:
+        PLAN["order"] = plan(ops)[0]
+    order = PLAN["order"]
+    at = {k: j for j, k in enumerate(order)}
+    last = set(max(gr, key=lambda k: at[k]) for gr in groups)
+    queue = {"V": g.vector, "S": g.scalar, "P": g.tensor, "G": g, "Y": g.sync}
+    known = {e: {} for e in queue}
+    snap, waits, marked = {}, {}, set()
+    for k in order:
+        o = ops[k]
+        kn = known[o["eng"]]
+        ws = []
+        for d in sorted(o["deps"], key=lambda d: -at[d]):
+            p = ops[d]
+            if p["sem"] is None and p["eng"] == "P" and o["eng"] == "P":
+                continue
+            key = p["sem"][0] if p["sem"] is not None else p["eng"]
+            if kn.get(key, -1) >= at[d]:
+                continue
+            ws.append(d)
+            if p["sem"] is None:
+                marked.add(d)
+            kn[key] = at[d]
+            for x, v in snap[d].items():
+                if kn.get(x, -1) < v:
+                    kn[x] = v
+        waits[k] = ws
+        snap[k] = dict(kn)
+    count, tick = {e: 0 for e in queue}, {}
+    for k in order:
+        o = ops[k]
+        e = o["eng"]
+        q = queue[e]
+        for d in waits[k]:
+            p = ops[d]
+            if p["sem"] is not None:
+                q.wait_ge(T.sem[p["sem"][0]], p["sem"][1])
+            else:
+                q.wait_ge(T.sem["e" + p["eng"]], tick[d])
+        ins = o["fn"](q, k in last) if e == "P" else o["fn"](q)
+        if o["sem"] is not None:
+            if o["sem"][0].startswith("d_"):
+                ins.then_inc(T.sem[o["sem"][0]], 16)
+        elif k in marked:
+            count[e] += 1
+            tick[k] = count[e]
+            ins.then_inc(T.sem["e" + e], 1)
+    for n in ("yx", "yl", "yz", "ya"):
+        for h in range(2):
+            g.sync.wait_ge(T.sem["d_%s%d" % (n, h)], 16)
+    g.wait_ge(T.sem.sent, sent)

@@ -5,84 +5,74 @@ from concourse.mybir import AluOpType, AxisListType, ActivationFunctionType
 N, W, LN, RO, BL = 8, 4096, 32, 3, 4
 DIST = [1 + (l // BL) % (N - 1) for l in range(LN)]
 HOPS = [DIST[BL * b] for b in range(LN // BL)] + [DIST[LN - 1] + 1]
-NB = 14
-MASK_S = True
+NF = 6
+SLOT = 2 * NF
+SET = SLOT * len(HOPS)
+RUN = 17
+WALKS = ((0, 12, 2), (12, 16, 4))
+SPLIT = ()
+ZW = 16 * (16 + len(WALKS))
+ZP = [0, 16 * (WALKS[0][1] + 1) * WALKS[0][2]]
+ZP.append(ZP[1] + 16 * (17 - WALKS[1][0]) * WALKS[1][2])
+ON_V = (0, 2, 4, 6, 9)
+FINE = [(r, h) for r in range(RO) for h in range(2)]
+EARLY = [(r, h) for r in range(RO) for h in range(2)]
 YOFF = 1536.0
-K0 = 32.0 * (32 - 40 * 4096)
+SQ = 592
 
 SCRATCH = {
-    "at8": ("sbuf", [128, 40], "int32"), "af8": ("sbuf", [128, 40], "float32"),
-    "ci": ("sbuf", [128, 8], "int32"), "cf": ("sbuf", [128, 16], "float32"),
-    "iob": ("sbuf", [128, 144], "bfloat16"), "ia": ("sbuf", [128, 256], "bfloat16"), "ib": ("sbuf", [128, 256], "bfloat16"),
-    "tci": ("sbuf", [128, 16], "int32"), "tcf": ("sbuf", [128, 20], "float32"),
-    "pk": ("sbuf", [128, 2048], "float16"), "swp": ("sbuf", [128, 128], "float16"), "mrg": ("sbuf", [128, 64], "float32"),
-    "bw1": ("sbuf", [128, 144], "bfloat16"), "bw2": ("sbuf", [128, 144], "bfloat16"), "bwn": ("sbuf", [128, 144], "bfloat16"),
-    "bwc": ("sbuf", [128, 144], "bfloat16"), "uw": ("sbuf", [128, 144], "bfloat16"),
-    "gio": ("sbuf", [128, 128], "bfloat16"), "blk": ("sbuf", [128, 128], "bfloat16"), "blk32": ("sbuf", [128, 128], "float32"),
-    "gi2": ("sbuf", [128, 128], "bfloat16"), "blk2": ("sbuf", [128, 128], "bfloat16"),
-    "ublk": ("sbuf", [128, 128], "float16"), "nb": ("sbuf", [128, 128], "bfloat16"), "nbt": ("sbuf", [128, 128], "bfloat16"),
-    "ra": ("sbuf", [128, 256], "float16"), "ri": ("sbuf", [128, 256], "float16"),
-    "rib": ("sbuf", [128, 256], "bfloat16"), "hw": ("sbuf", [128, 256], "bfloat16"), "rst": ("sbuf", [128, 256], "bfloat16"),
-    "bdo": ("sbuf", [128, 8], "uint16"), "lof": ("sbuf", [128, 2], "uint16"), "diag": ("sbuf", [128, 16], "float32"),
-    "kp": ("sbuf", [128, 32], "float16"), "kp2": ("sbuf", [128, 32], "float32"),
-    "one": ("sbuf", [128, 128], "bfloat16"), "c20": ("sbuf", [128, 256], "bfloat16"),
-    "snd": ("sbuf", [128, 480], "float32"), "rcv": ("sbuf", [128, 480], "float32"),
+    "at8": ("sbuf", [128, 40], "int32"), "af8": ("sbuf", [128, 40], "float16"),
+    "ci": ("sbuf", [128, 8], "int32"), "cf": ("sbuf", [128, 24], "float32"),
+    "tci": ("sbuf", [128, 16], "int32"), "tcf": ("sbuf", [128, 16], "float32"), "diag": ("sbuf", [128, 16], "float32"),
+    "k32": ("sbuf", [128, 16], "float32"), "lof": ("sbuf", [128, 8], "uint16"), "rep": ("sbuf", [128, 16], "uint16"),
+    "msg": ("sbuf", [128, 4 * RO * SET], "float32"),
 }
+for _n, _s in (("iob", 144), ("pk", 2048), ("pi", 2048), ("pick", 256), ("blk", 128), ("blk2", 128), ("ublk", 128), ("bw1", 144), ("uw", 144),
+               ("par", 1024), ("b9", 8 * RUN), ("wx", 8 * RUN), ("wm", 8 * RUN), ("sp", 8 * RUN + ZW), ("sa", 8 * RUN + ZW), ("sb", 8 * RUN + ZW),
+               ("r2", 32), ("kp", 32), ("rst", 256), ("sel", 256),
+               ("hwl", 256), ("hwh", 256), ("one", 128), ("c20", 256)):
+    SCRATCH[_n] = ("sbuf", [128, _s], "bfloat16")
 for _h in "01":
-    for _n, _s, _d in (("tab", W, "bfloat16"), ("lsb", 32, "int32"), ("zsb", 32, "bfloat16"), ("sel", 128, "float32"),
-                       ("cin", 64, "float32"), ("col", 8, "float32"), ("hot", 2, "bfloat16"), ("yb", 32, "bfloat16"),
-                       ("plu", 2, "uint16"), ("ot", 96, "float32"), ("of", 64, "float32"), ("oz", 32, "bfloat16"),
-                       ("lm", 16, "int32"), ("li", 16, "int32"), ("lc", 16, "float32"), ("zl", 32, "float16"), ("bd", 128, "float16"),
-                       ("las", 256, "float32"), ("w1", 256, "float32"), ("zr", 256, "bfloat16"), ("sm", 256, "float32"),
-                       ("q", 256, "float32"), ("wi", 256, "int32"), ("e0", 256, "int32"), ("eu", 256, "uint16"),
-                       ("gg", 4096, "bfloat16"), ("mx", 4096, "bfloat16"), ("mask", 256, "bfloat16"),
-                       ("si", 200, "int32"), ("offs", 2, "uint16"), ("winu", 16, "uint16"),
-                       ("xh", 256, "bfloat16"), ("ms", 256, "bfloat16"), ("yh", 16, "float16")):
+    for _n, _s, _d in (("tab", W, "bfloat16"), ("lsb", 32, "int32"), ("zsb", 32, "bfloat16"),
+                       ("cin", 32, "float32"), ("col", 8, "float32"), ("hot", 2, "bfloat16"), ("yb", 32, "bfloat16"),
+                       ("plu", 2, "uint16"), ("of", 64, "float32"), ("oz", 32, "bfloat16"), ("zl", 48, "float16"),
+                       ("w1", 256, "float32"), ("q", 256, "float32"), ("wi", 256, "int32"), ("e0", 256, "int32"), ("eu", 256, "uint16"),
+                       ("gg", 16 * ZW, "bfloat16"), ("mn", 16 * ZW, "bfloat16"), ("mask", 256, "bfloat16"),
+                       ("zs", 16, "bfloat16"), ("zt", 16, "float16"), ("zp", ZP[2], "bfloat16"),
+                       ("sm", 112, "float32"), ("si", 184, "int32"), ("offs", 4, "uint16"), ("winu", 16, "uint16"),
+                       ("xh", 256, "bfloat16"), ("ms", 256, "bfloat16"), ("yh", 32, "float16")):
         SCRATCH[_n + _h] = ("sbuf", [128, _s], _d)
-    for _n in ("pzl", "pd", "pm", "pll"):
+    for _n in ("pr", "pb", "pd", "pz"):
         SCRATCH[_n + _h] = ("psum", [128, 512], "float32")
 
-SEMAPHORES = (["eV", "eS", "eP", "eG", "sent", "d_an", "d_th"]
+SEMAPHORES = (["eV", "eS", "eP", "eG", "d_an", "d_th"]
               + ["d_%s%d" % (n, h) for n in ("xa", "xb", "la", "lb", "za", "zb", "yx", "yl", "ya", "yz") for h in range(2)]
-              + ["a%d%d" % (r, h) for r in range(RO) for h in range(2)])
+              + [n + "%d%d" % (r, h) for n in "as" for r in range(RO) for h in range(2)])
 
 A = AluOpType
 F = ActivationFunctionType
 X = AxisListType.X
-CASES = np.array([[1.04, 0.90, 1.20, 1.04], [1.35, 1.00, 1.70, 1.60], [0.52, 0.45, 0.60, 0.52], [10.0, 0.0, 20.0, 0.0], [30.0, 10.0, 60.0, 30.0],
-                  [70.0, 40.0, 100.0, 60.0], [130.0, 80.0, 200.0, 100.0], [2000.0, 1500.0, 2500.0, 2000.0], [4000.0, 2500.0, 6000.0, 5000.0]])
+CASES = np.array([[1.04, 0.92, 1.20, 1.00], [1.60, 1.20, 2.20, 1.35], [0.52, 0.46, 0.60, 0.52], [20.0, 20.0, 30.0, 50.0], [30.0, 30.0, 60.0, 60.0],
+                  [70.0, 150.0, 100.0, 60.0], [130.0, 220.0, 200.0, 100.0], [2000.0, 2000.0, 2500.0, 1500.0], [3000.0, 2500.0, 5000.0, 3500.0]])
 CV, CI, CP, FV, FS, LAT_SAME, LAT_X, LAT_DMA, LAT_REM = CASES
-PASSES, TRIES, FRESH = 4, 300, 40
-SG, XH_V = 2, False
-CUTS = ((0, 64), (64, 256))
+PASSES, TRIES, FRESH = 4, 120, 40
 PLAN = {}
 
 
+def level(j):
+    return 2.0 ** (8 * j - 64)
+
+
 def engine_split(topo, src, dsts):
-    off = [j for j, d in enumerate(dsts) if topo.chip(d) != topo.chip(src)]
-    on = [j for j, d in enumerate(dsts) if topo.chip(d) == topo.chip(src)]
-    out, used = {}, []
-    for part in (off, on):
-        if not part:
-            continue
-        pool = [e for e in topo.engines(src, dsts[part[0]]) if e not in used and all(e in topo.engines(src, dsts[j]) for j in part)]
-        size = [1] * len(part)
-        grow = True
-        while grow:
-            j = size.index(min(size))
-            grow = sum(size) + size[j] <= len(pool)
-            if grow:
-                size[j] *= 2
-        at = 0
-        for j, s in zip(part, size):
-            out[j] = pool[at:at + s]
-            at += s
-        used = used + pool
+    out = {}
+    for j in sorted(range(len(dsts)), key=lambda j: len(topo.engines(src, dsts[j]))):
+        free = [e for e in topo.engines(src, dsts[j]) if e not in out.values()]
+        out[j] = free[0] if topo.chip(dsts[j]) != topo.chip(src) else free[-1]
     return out
 
 
 def build(T, topo, rank):
-    ops, res, banks, groups, sent = [], {}, {}, [], [0]
+    ops, res, banks, groups = [], {}, {}, []
 
     def op(eng, fn, r, w, cost, bank=None, sem=None, acc=None, lat=0.0):
         k = len(ops)
@@ -107,7 +97,7 @@ def build(T, topo, rank):
             deps.update(b[2])
             b[1].append(k)
         deps.discard(k)
-        ops.append({"eng": eng, "fn": fn, "deps": deps, "cost": cost, "sem": sem, "lat": lat})
+        ops.append({"eng": eng, "fn": fn, "deps": deps, "cost": cost, "sem": sem, "lat": lat, "name": (list(w) + [acc])[0]})
         return k
 
     def n_of(ap):
@@ -116,8 +106,8 @@ def build(T, topo, rank):
             n *= s
         return n
 
-    def ts(out, in0, s1, s2, o0, o1, r, w, bank=None, half=False):
-        c = max(64, n_of(out) * (0.5 if half else 1)) * CV + FV
+    def ts(out, in0, s1, s2, o0, o1, r, w, bank=None, half=False, ind=False):
+        c = 50 + n_of(out) * CI if ind else max(64, n_of(out) * (0.5 if half else 1)) * CV + FV
         if o1 is None:
             return op("V", lambda e: e.tensor_scalar(out, in0, s1, None, o0), r, w, c, bank)
         return op("V", lambda e: e.tensor_scalar(out, in0, s1, s2, o0, o1), r, w, c, bank)
@@ -130,15 +120,17 @@ def build(T, topo, rank):
     def cp(out, a, r, w, bank=None, c=None):
         return op("V", lambda e: e.tensor_copy(out, a), r, w, c or max(64, n_of(out)) * CV + FV, bank)
 
-    def red(out, a, o, r, w, bank=None, neg=False):
-        return op("V", lambda e: e.tensor_reduce(out, a, X, o, negate=neg), r, w, 64 * CV + FV, bank)
+    def scan(out, a, b, o0, o1, r, w, bank=None):
+        c = max(64, n_of(out) * (1 if bank else 0.5)) * CV + FV
+        return op("V", lambda e: e.tensor_tensor_scan(out, a, b, 0.0, o0, o1), r, w, c, bank)
 
-    def act(out, a, f, r, w, bias=0.0, scale=1.0, bank=None, ind=False, accum=None):
+    def act(out, a, f, r, w, bias=0.0, scale=1.0, bank=None, ind=False):
         n = n_of(out)
         c = 65 + n * CI if ind else max(64, n) * CV + FS
-        if accum is not None:
-            return op("S", lambda e: e.activation(out, a, f, bias, scale, accum_out=accum), r, w, c + 20, bank)
         return op("S", lambda e: e.activation(out, a, f, bias, scale), r, w, c, bank)
+
+    def gcp(out, a, r, w):
+        return op("G", lambda e: e.affine_select(out, a, [[0, n_of(out)]], A.is_ge, 0.0, 0, 0), r, w, 170 + 2 * n_of(out) * CV)
 
     def fill(ap, v, w):
         return iota(ap, [[0, n_of(ap)]], int(v), 0, w)
@@ -163,302 +155,331 @@ def build(T, topo, rank):
     def dma(q, out, a, r, w, sem, lat):
         return op(q, lambda e: e.dma_start(out, a), r, w, 100.0, sem=(sem, 16), lat=lat)
 
-    def exchange(r, h, reads):
-        b, name, me = 80 * (2 * r + h), "a%d%d" % (r, h), T.cores[rank]
+    def base(r, h):
+        return 2 * SET * (2 * r + h)
+
+    def field(r, h, f, came=False, pair=False, lo=0, hi=16):
+        b = base(r, h) + (SET if came else 0) + (SLOT if pair else 0) + f
+        return T.msg[:, b + lo * NF:b + (hi - 1) * NF + 1:NF]
+
+    def sent_keys(r, h):
+        return [n + "%d%d" % (r, h) for n in ("sL", "sM", "sQ", "sA", "sLo", "sHi")]
+
+    def exchange(r, h):
+        b, name, me = base(r, h), "a%d%d" % (r, h), T.cores[rank]
         dst = [T.cores[(rank + d) % N] for d in HOPS]
         sp = engine_split(topo, me, dst)
-        trs, got = [], 0
+        trs, left = [], "s%d%d" % (r, h)
         for j, d in enumerate(dst):
             rid, pid, _ = topo.addr(d)
-            trs.append(RemoteDMATransfer(dst_ids=[DstId(rid=rid, pnc=pid)], dma_engine_mask=sum(1 << e for e in sp[j]), remote_sem=T.sem[name],
-                                         src=T.snd[:, b + 8 * j:b + 8 * j + 8], dst=T.rcv[:, b + 8 * j:b + 8 * j + 8]))
-            sent[0] += len(sp[j])
-            s = (rank - HOPS[j]) % N
-            got += len(engine_split(topo, T.cores[s], [T.cores[(s + e) % N] for e in HOPS])[j])
-        op("G", lambda e: e.remote_dma_fused(trs, local_sem=T.sem.sent), reads, ["rcv%d%d" % (r, h)], 1000.0, sem=(name, got), lat=LAT_REM)
+            a = b + SLOT * j
+            trs.append(RemoteDMATransfer(dst_ids=[DstId(rid=rid, pnc=pid)], dma_engine_mask=1 << sp[j], remote_sem=T.sem[name],
+                                         src=T.msg[:, a:a + SLOT], dst=T.msg[:, a + SET:a + SET + SLOT]))
+        wait = ["yx0"] if (r, h) == (RO - 1, 1) else []
+        k = op("G", lambda e: e.remote_dma_fused(trs, local_sem=T.sem[left]), sent_keys(r, h) + wait, ["rcv%d%d" % (r, h)], 1000.0,
+               sem=(name, len(HOPS)), lat=LAT_REM)
+        ops[op("Z", None, [], [left], 0.0, sem=(left, len(HOPS)), lat=LAT_REM - 1000)]["after"] = k
 
     dma("S", T.at8[0:8, 0:32], T.an[:], [], ["an"], "d_an", LAT_DMA)
     dma("S", T.at8[0:8, 32:33], T.th[:], [], ["th"], "d_th", LAT_DMA)
     prev = None
     for h in range(2):
         s = str(h)
-        for n, src, buf, q, lat in (("l", T.ls, "lsb", "Y", LAT_DMA), ("z", T.z, "zsb", "S", LAT_DMA), ("x", T.x, "tab", "Y", LAT_DMA + 3500 * (h + 1))):
+        for n, src, buf, q, lat in (("l", T.ls, "lsb", "Y", LAT_DMA), ("z", T.z, "zsb", "S", LAT_DMA), ("x", T.x, "tab", "Y", LAT_DMA + 3500)):
             for c in range(2):
-                k = dma(q, T[buf + s][64 * c:64 * c + 64, :], src[64 * h:64 * h + 64, :], [], [buf + s + "ab"[c]], "d_" + n + "ab"[c] + s, lat)
+                wait = ["tab0a", "tab0b"] if (n, h) == ("x", 1) else []
+                k = dma(q, T[buf + s][64 * c:64 * c + 64, :], src[64 * h:64 * h + 64, :], wait, [buf + s + "ab"[c]], "d_" + n + "ab"[c] + s, lat)
                 if q == "Y":
                     if prev is not None:
                         ops[k]["after"] = prev
                     prev = k
 
     cf = T.cf
-    gcol, fcol, g4col, c2col, ecol, ocol, mcol = [cf[:, j:j + 1] for j in range(7)]
-    g15, wcol, lane, scol = [cf[:, j:j + 1] for j in range(7, 11)]
+    c2col, gcol, fcol, g4col, ocol, last2, pcol = [cf[:, j:j + 1] for j in range(1, 8)]
+    g15, wcol, l2, top, lim, ndel, nb2, lo = [cf[:, j:j + 1] for j in range(8, 16)]
     iota(T.ci[:, 7:8], [[0, 1]], 0, 1, ["p"], True)
     iota(T.tci[:], [[-1, 16]], 16, 1, ["tci"], True)
     iota(T.iob[:], [[1, 144]], 0, 0, ["iob"])
-    iota(T.gio[:], [[16, 8], [0, 16]], 0, 0, ["gio"])
-    iota(T.ia[:], [[1, 16], [1, 16]], 0, 0, ["ia"])
-    iota(T.ib[:], [[1, 16], [0, 16]], 0, 0, ["ib"])
+    iota(T.blk[:], [[16, 8], [0, 16]], 0, 0, ["blk"])
     for h in range(2):
-        iota(T["sel%d" % h][0:8, :], [[0, 2], [1, 4], [0, 16]], 4 * h, -1, ["sel%d" % h])
-    iota(T.rst[:], [[0, 256]], 1, 0, ["rst"])
-    iota(T.gi2[:], [[0, 2], [16, 4], [0, 16]], 0, 0, ["gi2"])
+        iota(T.sel[0:8, 128 * h:128 * h + 128], [[0, 2], [1, 4], [0, 16]], 4 * h, -1, ["sel%d" % h])
+    iota(T.sa[:, 0:8 * RUN], [[0, 8], [1, RUN]], 0, 0, ["sa0"])
+    for x, (a, b, _) in enumerate(WALKS):
+        iota(T.sa[:, 8 * RUN + 16 * (a + x):8 * RUN + 16 * (b + x + 1)], [[0, 16], [1, b - a + 1]], 0, 0, ["sa%d" % (x + 1)])
+    fill(T.one[:], 1, ["one"])
+    fill(T.c20[0:1, :], 2080, ["c20"])
+    iota(T.b9[:], [[16, 8], [0, RUN]], 0, 0, ["b9"])
+    iota(T.kp[0:1, :], [[0, 2], [-1, 16]], 143, 0, ["kp"])
+    iota(T.hwl[:], [[0, 16], [1, 16]], 0, 0, ["hwl"])
+    iota(T.blk2[:], [[0, 2], [16, 4], [0, 16]], 0, 0, ["blk2"])
+    iota(T.pick[:], [[64, 2], [0, 2], [1, 64]], 0, 0, ["pick"])
+    fill(T.k32[:], 32, ["k32"])
     p = T.ci[:, 7:8]
-    for j, m in ((0, 0x70), (1, 15), (2, 0x30), (4, 14), (5, 1), (6, 63)):
+    for j, m in ((2, 0x70), (3, 15), (4, 0x30), (5, 1), (6, 14)):
         ts(T.ci[:, j:j + 1], p, m, None, A.bitwise_and, None, ["p"], ["p%d" % j])
-    ts(T.ci[:, 3:4], p, 5, 2, A.arith_shift_right, A.bitwise_and, ["p"], ["p3"])
-    cp(cf[:, 0:7], T.ci[:, 0:7], ["p%d" % j for j in range(7)], ["cf"])
+    ts(T.ci[:, 1:2], p, 5, 2, A.arith_shift_right, A.bitwise_and, ["p"], ["p1"])
+    cp(cf[:, 1:8], T.ci[:, 1:8], ["p"] + ["p%d" % j for j in range(1, 7)], ["cf"])
     ts(T.tci[:], T.tci[:], 15, None, A.bitwise_and, None, ["tci"], ["tci"])
-    ts(T.tcf[:, 0:16], T.tci[:], gcol, None, A.add, None, ["tci", "cf"], ["tcf"])
+    ts(T.tcf[:], T.tci[:], gcol, None, A.add, None, ["tci", "cf"], ["tcf"])
+    ts(T.blk[:], T.blk[:], gcol, None, A.is_equal, None, ["blk", "cf"], ["blk"], half=True)
+    ts(T.diag[:], T.iob[:, 0:16], fcol, None, A.is_equal, None, ["iob", "cf"], ["diag"])
     for k in range(16):
         ts(T.pk[:, 128 * k:128 * k + 128], T.iob[:, 0:128], T.tcf[:, k:k + 1], None, A.is_equal, None, ["iob", "tcf"], ["pk%d" % k], half=True)
+        if k % 2:
+            ts(T.pi[:, 128 * k:128 * k + 128], T.blk[:], T.diag[:, k:k + 1], None, A.mult, None, ["blk", "diag"], ["pi%d" % k], half=True)
+        else:
+            act(T.pi[:, 128 * k:128 * k + 128], T.blk[:], F.Identity, ["blk", "diag"], ["pi%d" % k], scale=T.diag[:, k:k + 1])
+    act(l2, last2, F.Identity, ["cf"], ["l2"], bias=ocol, scale=2.0)
+    ts(T.lof[:, 0:1], l2, c2col, None, A.add, None, ["cf", "l2"], ["lof"])
+    for c in range(2):
+        act(cf[:, 17 + c:18 + c], l2, F.Identity, ["l2"], ["lbase%d" % c], bias=256.0 * c, scale=128.0)
+    cp(T.rep[:], T.iob[:, 0:16], ["iob"], ["rep"])
     act(g15, gcol, F.Identity, ["cf"], ["g15"], bias=15.0)
     act(wcol, fcol, F.Identity, ["cf"], ["wcol"], bias=1.0, scale=2.0)
-    act(cf[:, 11:12], ecol, F.Identity, ["cf"], ["l0"], bias=ocol, scale=2.0)
-    act(lane, cf[:, 11:12], F.Identity, ["cf", "l0"], ["lane"], bias=c2col)
-    act(cf[:, 12:13], lane, F.Identity, ["lane"], ["pb0"], scale=128.0)
-    act(cf[:, 14:15], c2col, F.Identity, ["cf"], ["l1"], bias=256.0, scale=-256.0)
-    act(cf[:, 13:14], cf[:, 14:15], F.Identity, ["l1", "pb0"], ["pb1"], bias=cf[:, 12:13])
-    act(cf[:, 15:16], c2col, F.Identity, ["cf"], ["l2"], bias=64.0, scale=-32.0)
-    act(scol, cf[:, 15:16], F.Identity, ["cf", "l2"], ["scol"], bias=mcol)
-    cp(T.lof[:, 0:1], lane, ["lane"], ["lof"])
-    ts(T.swp[:], T.iob[:, 0:128], scol, None, A.is_equal, None, ["iob", "scol"], ["swp"], half=True)
-    ts(T.mrg[:], T.iob[:, 0:64], mcol, None, A.is_equal, None, ["iob", "cf"], ["mrg"])
-    ts(T.blk[:], T.gio[:], gcol, None, A.is_equal, None, ["gio", "cf"], ["blk"], half=True)
-    ts(T.blk2[:], T.gi2[:], g4col, None, A.is_equal, None, ["gi2", "cf"], ["blk2"], half=True)
-    ts(T.bdo[:], T.iob[:, 0:8], 0.0, fcol, A.mult, A.add, ["iob", "cf"], ["bdo"])
-    ts(T.diag[:], T.iob[:, 0:16], fcol, None, A.is_equal, None, ["iob", "cf"], ["diag"])
-    act(T.tcf[:, 16:17], fcol, F.Identity, ["cf"], ["f8"], bias=-8.0, scale=-1.0)
-    act(T.ia[:], T.ia[:], F.Abs, ["ia", "f8"], ["ia"], bias=T.tcf[:, 16:17])
-    ts(T.ra[:], T.ia[:], 8.0, None, A.is_equal, None, ["ia"], ["ra"], half=True)
-    ts(T.ri[:], T.ib[:], fcol, None, A.is_equal, None, ["ib", "cf"], ["ri"], half=True)
-    ts(T.rib[:], T.ib[:], fcol, None, A.is_equal, None, ["ib", "cf"], ["rib"], half=True)
-    act(T.hw[:], T.rib[:], F.Identity, ["rib"], ["hw"], bias=-8192.0, scale=12288.0)
-    op("G", lambda e: e.affine_select(T.rst[:], T.rst[:], [[0, 16], [1, 16]], A.is_gt, 0.0, 0, 0), ["rst"], ["rst"], 170 + 512 * CV)
+    act(top, fcol, F.Identity, ["cf"], ["top"], bias=15.0, scale=16.0)
+    act(lim, T.diag[:, 0:1], F.Identity, ["diag"], ["lim"], bias=-1.0, scale=33.0)
+    act(ndel, T.diag[:, 0:1], F.Identity, ["diag"], ["ndel"], scale=-1.0)
+    act(nb2, T.diag[:, 0:1], F.Identity, ["diag"], ["nb2"], bias=-127.0, scale=0.5)
+    home = [2 * b for b in range(LN // BL) if (DIST[BL * b] + 1) % N == 0][0]
+    ts(lo, last2, float(home), -float(SET), A.is_equal, A.mult, ["cf"], ["lo0"])
+    act(lo, fcol, F.Identity, ["lo0", "cf"], ["lo0"], bias=lo, scale=float(NF))
+    ts(T.lof[:, 2:3], lo, float(SET + SLOT + 5), None, A.add, None, ["lo0"], ["lof1"])
+    a = 8 * RUN + 16 * (WALKS[0][1] + 1)
+    ts(T.sb[:, 0:a], T.sa[:, 0:a], 0.0, level(-1), A.is_equal, A.mult, ["sa0", "sa1"], ["sb0"], half=True)
+    ts(T.sb[:, a:], T.sa[:, a:], 0.0, level(WALKS[1][0] - 1), A.is_equal, A.mult, ["sa2"], ["sb1"], half=True)
+    ts(T.sa[:], T.sa[:], 0.0, 256.0, A.is_gt, A.mult, [], ["sa0", "sa1", "sa2"], half=True)
+    scan(T.sp[:], T.sa[:], T.sb[:], A.mult, A.max, ["sa0", "sb0", "sb1"], ["sp"])
+    ts(T.b9[:], T.b9[:], gcol, 256.0, A.is_equal, A.mult, ["b9", "cf"], ["b9"], half=True)
+    tt(T.wx[:], T.b9[:], T.sp[:, 0:8 * RUN], A.mult, ["b9", "sp"], ["wx"])
+    act(T.wm[:], T.wx[:], F.Identity, ["wx"], ["wm"], scale=-2.0)
+    for g in range(8):
+        ts(T.par[:, 128 * g:128 * g + 128], T.one[:], T.blk[:, 16 * g:16 * g + 1], None, A.mult, None, ["one", "blk"], ["par%d" % g], half=True)
+    act(T.r2[:, 0:16], T.diag[:], F.Identity, ["diag"], ["r2a"], scale=8.0)
+    act(T.r2[:, 16:32], T.diag[:], F.Identity, ["diag"], ["r2b"], scale=-8.0)
+    ts(T.rst[:], T.hwl[:], 0.0, None, A.is_gt, None, ["hwl"], ["rst"], half=True)
+    ts(T.hwl[:], T.hwl[:], fcol, 6144.0, A.is_equal, A.mult, ["hwl", "cf"], ["hwl"], half=True)
+    ts(T.hwh[:], T.hwl[:], -1.0, 12288.0, A.mult, A.add, ["hwl"], ["hwh"], half=True)
+    ts(T.blk2[:], T.blk2[:], g4col, 0.5, A.is_equal, A.mult, ["blk2", "cf"], ["blk2"], half=True)
+    ts(T.pick[:], T.pick[:], pcol, None, A.is_equal, None, ["pick", "cf"], ["pick"], half=True)
     ts(T.bw1[:], T.iob[:], g15, None, A.is_equal, None, ["iob", "g15"], ["bw1"], half=True)
-    act(T.bw2[:], T.bw1[:], F.Identity, ["bw1"], ["bw2"], scale=2.0)
-    act(T.bwn[:], T.bw1[:], F.Identity, ["bw1"], ["bwn"], scale=-1.0)
-    if MASK_S:
-        act(T.bwc[:], T.bw1[:], F.Identity, ["bw1"], ["bwc"], scale=128.0)
     act(T.uw[:], T.bw1[:], F.Identity, ["bw1", "wcol"], ["uw"], scale=wcol)
     ts(T.ublk[:], T.blk[:], wcol, None, A.mult, None, ["blk", "wcol"], ["ublk"], half=True)
-    act(T.blk32[:], T.blk[:], F.Identity, ["blk"], ["blk32"])
-    act(T.nbt[:], T.blk[:], F.Identity, ["blk"], ["nbt"], scale=-1.0)
-    op("G", lambda e: e.affine_select(T.nb[:], T.nbt[:], [[0, 8], [-1, 16]], A.is_ge, 0.0, NB - 1, 0), ["nbt"], ["nb"], 170 + 256 * CV)
-    ts(T.kp[:, 0:16], T.iob[:, 0:16], -16.0, 2048.0 if MASK_S else 0.0, A.mult, A.add, ["iob"], ["kp"])
-    ts(T.kp[:, 16:17], T.iob[:, 0:1], 16384.0, None, A.add, None, ["iob"], ["kpe"])
-    fill(T.kp2[:, 0:16], -32.0, ["kp2"])
-    fill(T.kp2[:, 16:17], 480.0, ["kp3"])
-    act(T.one[0:1, :], T.iob[0:1, 0:128], F.Identity, ["iob"], ["one"], bias=1.0, scale=0.0)
-    act(T.c20[0:1, :], T.ib[0:1, :], F.Identity, ["ib"], ["c20"], bias=2080.0, scale=0.0)
-    fill(T.snd[:], 0.0, ["snd"])
-    cp(T.af8[0:8, 0:33], T.at8[0:8, 0:33], ["an", "th"], ["af8"])
+    act(T.af8[0:8, 0:33], T.at8[0:8, 0:33], F.Identity, ["an", "th"], ["af8"], bias=-2048.0)
     for h in range(2):
         s = str(h)
-        sel = T["sel" + s][0:8, :]
-        ts(sel, sel, 0.0, None, A.is_equal, None, ["sel" + s], ["sel" + s])
-        px = T["pm" + s]
-        mm(px[:, 200:233], sel, T.af8[0:8, 0:33], ["sel" + s, "af8"], "pxb" + s, "pm" + s, True, f32=True)
-        act(T["cin" + s][:, 0:32], px[:, 200:232], F.Identity, ["pxb" + s], ["cin" + s], bias=32.0 * (32 - W), scale=32.0, bank="pm" + s)
-        act(T["col" + s][:, 0:1], px[:, 232:233], F.Identity, ["pxb" + s], ["tcol" + s], bias=-0.5, bank="pm" + s)
-        fill(T["ot" + s][:], 0.0, ["ot0" + s, "ot1" + s, "ot2" + s])
+        sel = T.sel[0:8, 128 * h:128 * h + 128]
+        ts(sel, sel, 0.0, None, A.is_equal, None, ["sel" + s], ["sel" + s], half=True)
+        px = T["pz" + s]
+        mm(px[:, 0:33], sel, T.af8[0:8, 0:33], ["sel" + s, "af8"], "px" + s, "pz" + s, True)
+        act(T["cin" + s][:], px[:, 0:32], F.Identity, ["px" + s], ["cin" + s], bias=32.0 * (32 - 2048), scale=32.0, bank="pz" + s)
+        act(T["col" + s][:, 0:1], px[:, 32:33], F.Identity, ["px" + s, "ndel", "nb2"], ["nb0" + s], bias=nb2, scale=ndel, bank="pz" + s)
+        for x, (lo_, hi, rep) in enumerate(WALKS):
+            fill(T["gg" + s][:, 256 * (lo_ + x):256 * (hi + x + 1):hi - lo_ + 1], 0, ["gz%s%d" % (s, x)])
+    for r in range(RO):
+        for h in range(2):
+            fill(T.msg[:, base(r, h):base(r, h) + SET], 0, sent_keys(r, h))
 
-    def lists(r, h):
-        b, s = 80 * (2 * r + h), str(h)
-        lm = T["lm" + s]
-        own = [j for j in range(LN // BL) if (DIST[BL * j] + 1) % N == 0]
-        cuts = [0] + [c for j in own for c in (2 * j, 2 * j + 2)] + [16]
-        for j in range(len(cuts) - 1):
-            lo, hi = cuts[j], cuts[j + 1]
-            src = T.snd if j % 2 else T.rcv
-            tt(lm[:, lo:hi], T.rcv[:, b + 4 * lo:b + 4 * hi:4], src[:, b + 11 + 4 * lo:b + 8 + 4 * hi:4], A.max,
-               ["rcv%d%d" % (r, h), "sP%d%d" % (r, h)], ["lm%s_%d" % (s, j)])
-        ts(T["li" + s][:], lm[:], W - 1, None, A.bitwise_and, None, ["lm%s_%d" % (s, j) for j in range(len(cuts) - 1)], ["li" + s])
+    def unfold(out, lt, step, src, n, r, key, bank):
+        keys = []
+        for c in range(2):
+            for u in range(2):
+                keys.append("%s_%d%d" % (key, c, u))
+                mm(out[0:64, 2 * c + u:2 * n:4], lt[:, step * c:step * c + 64], src[:, u:n:2], r, keys[-1], bank, True)
+        return keys
+
+    def arrive(r, h):
+        s, rh = str(h), "%d%d" % (r, h)
+        t = lambda n: T[n + s]
+        sm, si, key = t("sm"), t("si"), "rcv" + rh
+        win = T.msg[:, base(r, h):base(r, h) + 2 * SET]
+        kw = [key] + sent_keys(r, h)
+        for a, b in ((0, home), (home, home + 2), (home + 2, 16)):
+            tt(sm[:, a:b], field(r, h, 0, True, False, a, b), field(r, h, 4, a != home, True, a, b), A.max, kw, ["m%d%s" % (a, s)])
+        tt(t("zl")[:, 0:16], win.indirect(T.lof[:, 2:3]), sm[:, 0:16], A.min, kw + ["lof1"] + ["m%d%s" % (a, s) for a in (0, home, home + 2)],
+           ["zl" + s], ind=True)
+        mh, zq = field(r, h, 1, True), field(r, h, 2, True)
+        tt(t("yh")[:, 0:16], mh, zq, A.add, [key], ["yr" + s])
+        if r < RO - 1:
+            p, n, keys = 128, 16, ["pu" + s]
+            mm(t("pd")[:, 0:16], T.ublk[:], t("yh")[:, 0:16], ["ublk", "yr" + s], "pu" + s, "pd" + s, True)
+        else:
+            p, n = 64, 32
+            keys = unfold(t("pd"), T.ublk, 64, t("yh"), 16, ["ublk", "yr" + s], "pu" + s, "pd" + s)
+        act(si[0:p, 0:n], t("pd")[0:p, 0:n], F.Identity, keys, ["ui" + s], bank="pd" + s)
+        ts(si[0:p, 32:32 + n], si[0:p, 0:n], W - 1, None, A.bitwise_and, None, ["ui" + s], ["u" + s])
+        act(si[0:p, 152:152 + n], si[0:p, 32:32 + n], F.Square, ["u" + s], ["sq" + s], bias=float(SQ))
+        tt(sm[:, 48:64], zq, mh, A.subtract, [key], ["dz" + s])
+        z = sm[:, 32:48] if r < RO - 1 else t("zl")[:, 16:32]
+        act(z, sm[:, 48:64], F.Abs, ["dz" + s], ["z" + s], bias=0.5 - 2 * YOFF, scale=2.0)
 
     def prep(r, h):
-        s = str(h)
+        s, rh = str(h), "%d%d" % (r, h)
         t = lambda n: T[n + s]
-        sm, li, kl = t("sm"), t("li")[:], "li" + s
+        sm, si, zl, col = t("sm"), t("si"), t("zl")[:, 0:16], t("col")
+        z, c32 = sm[:, 32:48], sm[:, 64:80]
         if r == 0:
             lof = T.lof[:, 0:1]
-            cp(li, t("lsb")[:, 0:32].indirect(lof), ["lsb%sa" % s, "lsb%sb" % s, "lof"], [kl], c=80.0)
-            z, c32, kz, kc = t("cin")[:, 32:48], t("cin")[:, 48:64], "z0" + s, "c0" + s
-            act(z, t("zsb")[:, 0:32].indirect(lof), F.Identity, ["zsb%sa" % s, "zsb%sb" % s, "lof"], [kz], ind=True)
-            act(c32, t("cin")[:, 0:32].indirect(lof), F.Identity, ["cin" + s, "lof"], [kc], ind=True)
+            ts(zl, t("lsb")[:, 0:32].indirect(lof), -2048.0, None, A.add, None, ["lsb%sa" % s, "lsb%sb" % s, "lof"], ["zl" + s], ind=True)
+            act(z, t("zsb")[:, 0:32].indirect(lof), F.Identity, ["zsb%sa" % s, "zsb%sb" % s, "lof"], ["z" + s], ind=True)
+            act(c32, t("cin")[:, 0:32].indirect(lof), F.Identity, ["cin" + s, "lof"], ["c32" + s], ind=True)
+            act(t("zt")[:], z, F.Identity, ["z" + s, "nb0" + s], ["zt" + s], bias=col[:, 0:1])
         else:
-            lists(r - 1, h)
-            b = 80 * (2 * (r - 1) + h)
-            z, c32 = T.rcv[:, b + 1:b + 64:4], T.rcv[:, b + 2:b + 64:4]
-            kz = kc = "rcv%d%d" % (r - 1, h)
-        ts(t("lc")[:], li, -2048.0, None, A.add, None, [kl], ["lc" + s])
-        ts(t("zl")[:, 1:32:2], li, -2048.0, None, A.add, None, [kl], ["zlL" + s])
-        cp(t("zl")[:, 0:32:2], z, [kz], ["zlz" + s])
-        tt(t("bd")[:], t("lc")[:, 0:16].indirect(T.bdo[:, 0:8]), T.blk[:], A.mult, ["lc" + s, "bdo", "blk"], ["bd" + s], ind=True)
-        pll, kb = t("pll"), "pll" + s
-        pli = t("pd")[:, 256:512]
-        mm(pll[:, 0:256], t("bd")[:], T.ra[:], ["bd" + s, "ra"], "pLa" + s, kb, True)
-        mm(pli, T.one[0:1, :], T.c20[0:1, :], ["one", "c20"], "pLi" + s, "pd" + s, True)
-        mm(pli, t("bd")[:], T.ri[:], ["bd" + s, "ri"], "pLi" + s, "pd" + s, False)
-        for k in range(16):
-            mm(t("pzl")[:, 32 * k:32 * k + 32], T.pk[:, 128 * k:128 * k + 128], t("zl")[:], ["pk%d" % k, "zlL" + s, "zlz" + s],
-               "pzl%s_%d" % (s, k), "pzl" + s, True)
-        kzl = ["pzl%s_%d" % (s, k) for k in range(16)]
-        for j, (a, b) in enumerate(CUTS):
-            act(t("las")[:, a:b], pll[:, a:b], F.Identity, ["pLa" + s], ["las%s%d" % (s, j)], bias=2016.0, bank=kb)
-        act(t("zr")[:], t("pzl")[:, 0:512:2], F.Identity, kzl, ["zr" + s], bank="pzl" + s)
-        act(t("w1")[:], t("pzl")[:, 1:512:2], F.Identity, kzl, ["w1" + s], bias=2016.0, bank="pzl" + s)
-        act(sm[:, 0:16], t("lc")[:], F.Identity, ["lc" + s], ["F0" + s], bias=2080.0)
-        act(sm[:, 16:32], t("lc")[:], F.Identity, ["lc" + s], ["F1" + s], bias=2080.0)
-        act(sm[:, 32:48], z, F.Identity, [kz], ["zq" + s], bias=YOFF - 0.25, scale=0.5)
-        ccol = t("col")[:, 1:2]
-        tt(sm[:, 64:80], c32, T.diag[:], A.mult, [kc, "diag"], ["cd" + s])
-        act(sm[:, 80:96], sm[:, 64:80], F.Identity, ["cd" + s], ["ccol" + s], accum=ccol)
-        act(sm[:, 96:112], c32, F.Identity, [kc], ["c20" + s])
-        act(sm[:, 112:128], c32, F.Identity, [kc], ["c21" + s])
-        for j, (a, b) in enumerate(CUTS):
-            tt(t("q")[:, a:b], t("pd")[:, 256 + a:256 + b], t("las")[:, a:b], A.mult, ["pLi" + s, "las%s%d" % (s, j)], ["q%s%d" % (s, j)], bank="pd" + s)
-        for j, (a, b) in enumerate(CUTS):
-            ts(t("wi")[:, a:b], t("q")[:, a:b], ccol, None, A.add, None, ["q%s%d" % (s, j), "ccol" + s], ["wi%s%d" % (s, j)])
-            ts(t("e0")[:, a:b], t("wi")[:, a:b], 5, W - 1, A.arith_shift_right, A.bitwise_and, ["wi%s%d" % (s, j)], ["e0%s%d" % (s, j)])
-            cp(t("eu")[:, a:b], t("e0")[:, a:b], ["e0%s%d" % (s, j)], ["eu%s%d" % (s, j)])
+            arrive(r - 1, h)
+            ts(si[:, 48:64], si[:, 152:168], 32 * W - 32, None, A.bitwise_and, None, ["sq" + s], ["s" + s])
+            tt(c32, si[:, 48:64], field(r - 1, h, 3, True), A.add, ["s" + s, "rcv%d%d" % (r - 1, h)], ["c32" + s])
+            ts(t("zt")[:], z, col[:, 4:5], col[:, 0:1], A.subtract, A.add, ["z" + s, "am" + s, "nb0" + s], ["zt" + s])
+        pr, pb, pz = t("pr"), t("pb"), t("pz")
+        mm(pb[:, 0:256], T.one[0:1, :], T.c20[0:1, :], ["one", "c20"], "li" + s, "pb" + s, True)
+        for i in range(16):
+            mm(pr[:, i:256:16], T.pk[:, 128 * i:128 * i + 128], zl, ["pk%d" % i, "zl" + s], "la%s_%d" % (s, i), "pr" + s, True)
+        for i in range(16):
+            mm(pb[:, i:256:16], T.pi[:, 128 * i:128 * i + 128], zl, ["pi%d" % i, "zl" + s], "li" + s, "pb" + s, False)
+        cuts = ((0, 64, "a"), (64, 256, "b")) if (r, h) in EARLY else ((0, 256, "ab"),)
+        kc = lambda n, c: [n + s + x for x in c]
+        for a, b, c in cuts:
+            act(t("w1")[:, a:b], pr[:, a:b], F.Identity, ["la%s_%d" % (s, i) for i in range(16)], kc("w1", c), bias=2016.0, bank="pr" + s)
+        for a, b, c in cuts:
+            tt(t("q")[:, a:b], pb[:, a:b], t("w1")[:, a:b], A.mult, ["li" + s] + kc("w1", c), kc("q", c), bank="pb" + s)
+        for a, b, c in cuts:
+            tt(t("wi")[:, a:b], c32.indirect(T.rep[:, a // 16:b // 16]), t("q")[:, a:b], A.add, kc("q", c) + ["c32" + s, "rep"], kc("wi", c), ind=True)
+            ts(t("e0")[:, a:b], t("wi")[:, a:b], 5, W - 1, A.arith_shift_right, A.bitwise_and, kc("wi", c), kc("e0", c))
+            cp(t("eu")[:, a:b], t("e0")[:, a:b], kc("e0", c), kc("eu", c))
+        act(sm[:, 16:32], zl, F.Identity, ["zl" + s], ["F" + s], bias=2080.0)
+        act(field(r, h, 2), z, F.Identity, ["z" + s], ["sQ" + rh], bias=YOFF - 0.25, scale=0.5)
+        tt(t("zs")[:], z, T.sp[:, 1:RUN], A.mult, ["z" + s, "sp"], ["zs" + s])
+        mm(pz[:, 0:ZW], T.one[0:1, :], T.sp[0:1, 8 * RUN:8 * RUN + ZW], ["one", "sp"], "pz" + s, "pz" + s, True)
+        for x, (lo, hi, rep) in enumerate(WALKS):
+            for k in range(16):
+                a = 16 * (lo + x) + (hi - lo + 1) * k + 1
+                mm(pz[:, a:a + hi - lo], T.pk[:, 128 * k:128 * k + 128], t("zs")[:, lo:hi], ["pk%d" % k, "zs" + s], "pz" + s, "pz" + s, False)
+        a = ZP[1] - 16 * (WALKS[0][1] + 1)
+        act(t("zp")[:, a:a + ZW], pz[:, 0:ZW], F.Identity, ["pz" + s], ["zp%s%d" % (s, x) for x in range(2)], bank="pz" + s)
+        for x, (lo, hi, rep) in enumerate(WALKS):
+            n = 16 * (hi - lo + 1)
+            while n < 16 * (hi - lo + 1) * rep:
+                a = ZP[1] - n if x == 0 else ZP[1]
+                b = a - n if x == 0 else a + n
+                gcp(t("zp")[:, b:b + n], t("zp")[:, a:a + n], ["zp%s%d" % (s, x)], ["zp%s%d" % (s, x)])
+                n *= 2
 
     def gath(r, h):
         s = str(h)
         t = lambda n: T[n + s]
         win, kw = t("tab")[:, 0:W], ["tab%sa" % s, "tab%sb" % s]
-        kzl = ["pzl%s_%d" % (s, k) for k in range(16)]
-        pd = t("pd")[:, 0:256]
-        mm(pd, T.nb[:], t("zr")[:], ["nb", "zr" + s], "pd" + s, "pd" + s, True)
-        ch = lambda n, i, m=1: t(n)[:, 256 * i:256 * (i + m)]
-        sl = lambda n, i: T[n][:, 15 - i:143 - i]
-        piece = lambda i: ["eu%s%d" % (s, j) for j, (a, b) in enumerate(CUTS) if a <= 16 * i < b]
-        i = 0
-        while i < NB:
-            m = min(SG, NB - i)
-            act(ch("gg", i, m), win.indirect(t("eu")[:, 16 * i:16 * (i + m)]), F.Identity,
-                kw + piece(i) + piece(i + m - 1), ["gg%s_%d" % (s, j) for j in range(i, i + m)], ind=True)
-            i += m
-        for i in range(NB, 16):
-            tt(ch("gg", i), win.indirect(t("eu")[:, 16 * i:16 * i + 16]), t("zr")[:], A.subtract,
-               kw + piece(i) + ["zr" + s], ["gg%s_%d" % (s, i)], ind=True)
-            act(ch("mx", i), ch("gg", i), F.Abs, ["gg%s_%d" % (s, i)], ["mx%s_%d" % (s, i)])
-            mm(pd, sl("bw1", i), ch("mx", i), ["bw1", "mx%s_%d" % (s, i)], "pd" + s, "pd" + s, False)
-        for i in range(NB):
-            tt(ch("mx", i), ch("gg", i), t("pzl")[:, 0:512:2], A.max, ["gg%s_%d" % (s, i)] + kzl, ["mx%s_%d" % (s, i)], bank="pzl" + s)
-            mm(pd, sl("bwn", i), ch("gg", i), ["bwn", "gg%s_%d" % (s, i)], "pd" + s, "pd" + s, False)
-            mm(pd, sl("bw2", i), ch("mx", i), ["bw2", "mx%s_%d" % (s, i)], "pd" + s, "pd" + s, False)
+        fine = (r, h) in FINE
+        dist = [(t("pd"), 256, "d0" + s, "pd" + s), (t("pz"), 384, "d1" + s, "pz" + s) if fine else (t("pd"), 384, "d0" + s, "pd" + s)]
+        for ih, (d, a, key, bank) in enumerate(dist):
+            for g in range(8):
+                mm(d[:, a + 16 * g:a + 16 * g + 16], T.par[:, 128 * g:128 * g + 128], t("zt")[:], ["par%d" % g, "zt" + s], key, bank,
+                   g == 0 and (fine or ih == 0))
+        for x, (lo, hi, rep) in enumerate(WALKS):
+            run, at = hi - lo + 1, 256 * (lo + x)
+            col = lambda n, j, ih, w: t(n)[:, at + 128 * run * ih + 1 + j - lo:at + 128 * run * (ih + w):run]
+            for ih, w in (((0, 1), (1, 1)) if x in SPLIT else ((0, 2),)):
+                for j in range(lo, hi):
+                    src = win.indirect(t("eu")[:, 16 * j + 8 * ih:16 * j + 8 * (ih + w)])
+                    rd = kw + ["eu" + s + "ab"[j >= 4]]
+                    wr = ["gg%s_%d_%d" % (s, j, c) for c in range(ih, ih + w)]
+                    if j in ON_V:
+                        ts(col("gg", j, ih, w), src, level(j), level(j), A.mult, A.add, rd, wr, ind=True)
+                    else:
+                        act(col("gg", j, ih, w), src, F.Identity, rd, wr, bias=level(j), scale=level(j), ind=True)
+            for i in range(0, 16, rep):
+                a, n = at + 16 * run * i, 16 * run * rep
+                scan(t("mn")[:, a:a + n], t("gg")[:, a:a + n], t("zp")[:, ZP[x]:ZP[x] + n], A.max, A.min,
+                     ["gg%s_%d_%d" % (s, j, i // 8) for j in range(lo, hi)] + ["zp%s%d" % (s, x), "gz%s%d" % (s, x)],
+                     ["mn%s_%d_%d" % (s, x, c) for c in range(i, i + rep)])
+            for ih, (d, a, key, bank) in enumerate(dist):
+                for j in range(lo, hi):
+                    out = d[:, a + j:a + 128:16]
+                    mm(out, col("gg", j, ih, 1), T.wx[:, 16 - j:8 * RUN:RUN], ["wx", "gg%s_%d_%d" % (s, j, ih)], key, bank, False)
+                    mm(out, col("mn", j, ih, 1), T.wm[:, 16 - j:8 * RUN:RUN], ["wm"] + ["mn%s_%d_%d" % (s, x, i) for i in range(8 * ih, 8 * ih + 8)],
+                       key, bank, False)
+        if fine:
+            for ih, (d, a, key, bank) in enumerate(dist):
+                act(t("mask")[:, 128 * ih:128 * ih + 128], d[:, a:a + 128], F.Sign, [key], ["mask%s%d" % (s, ih)], scale=-1.0, bank=bank)
+        else:
+            act(t("mask")[:], t("pd")[:, 256:512], F.Sign, ["d0" + s], ["mask%s%d" % (s, ih) for ih in range(2)], scale=-1.0, bank="pd" + s)
 
     def counts(r, h):
-        s = str(h)
+        s, rh = str(h), "%d%d" % (r, h)
         t = lambda n: T[n + s]
-        si, sm, pm, col = t("si"), t("sm"), t("pm"), t("col")
-        thr, kt = (col[:, 0:1], "tcol" + s) if r == 0 else (col[:, 2:3], "thr" + s)
-        if MASK_S:
-            act(t("mask")[:], t("pd")[:, 0:256], F.Sign, ["pd" + s, kt], ["mask" + s], bias=thr, scale=-1.0, bank="pd" + s)
-        else:
-            ts(t("mask")[:], t("pd")[:, 0:256], thr, 256.0, A.is_lt, A.mult, ["pd" + s, kt], ["mask" + s], bank="pd" + s)
-        bw = "bwc" if MASK_S else "bw1"
-        mm(pm[:, 0:17], T.pk[:, 0:128], T.kp[:, 0:17], ["pk0", "kp", "kpe"], "pc" + s, "pm" + s, True)
-        for l in range(16):
-            mm(pm[:, 0:16], T[bw][:, 15 - l:143 - l], t("mask")[:, l:256:16], [bw, "mask" + s], "pc" + s, "pm" + s, False)
-        red(si[:, 175:176], pm[:, 0:16], A.max, ["pc" + s], ["n0" + s], bank="pm" + s, neg=True)
-        op("V", lambda e: e.tensor_tensor_scan(si[:, 176:193], T.kp2[:, 0:17], pm[:, 0:17], 65536.0, A.add, A.min),
-           ["pc" + s, "kp2", "kp3"], ["n1" + s], 64 * CV + FV, "pm" + s)
-        ts(si[:, 2:4], si[:, 175:193:17], 255, None, A.bitwise_and, None, ["n0" + s, "n1" + s], ["na" + s])
-        ts(t("offs")[:], si[:, 2:4], fcol, None, A.add, None, ["na" + s, "cf"], ["offs" + s])
-        ts(t("hot")[:, 0:1], si[:, 175:176], -2048.0, None, A.is_lt, None, ["n0" + s], ["hot" + s])
-        pa = pm[:, 64:65]
-        mm(pa, T.blk2[:], t("hot")[:, 0:1], ["blk2", "hot" + s], "pA" + s, "pm" + s, True)
+        si, pb, col = t("si"), t("pb"), t("col")
+        pk = pb[:, 256:288]
+        mm(pk, T.one[0:1, :], T.kp[0:1, :], ["one", "kp"], "pc" + s, "pb" + s, True)
+        for ih in range(2):
+            mm(pk, t("mask")[:, 128 * ih:128 * ih + 128], T.r2[:], ["r2a", "r2b", "mask%s%d" % (s, ih)], "pc" + s, "pb" + s, False)
+        scan(si[:, 64:96], T.rst[:, 0:32], pk, A.mult, A.max, ["pc" + s, "rst"], ["key" + s], bank="pb" + s)
+        ts(si[:, 96:98], si[:, 79:96:16], 15, None, A.bitwise_and, None, ["key" + s], ["na" + s])
+        ts(t("offs")[:, 0:4:2], si[:, 96:98], -1.0, top, A.mult, A.add, ["na" + s, "top"], ["offs" + s])
+        act(t("hot")[:, 0:1], si[:, 79:80], F.Sign, ["key" + s], ["hot" + s], bias=0.5 - 16 * 9)
+        pa = pb[:, 300:301]
+        mm(pa, T.blk2[:], t("hot")[:, 0:1], ["blk2", "hot" + s], "pA" + s, "pb" + s, True)
+        mm(pa, T.one[0:1, :], T.iob[0:1, 16:17], ["one", "iob"], "pA" + s, "pb" + s, False)
+        ts(field(r, h, 3), T.k32[:], pa, (1024.0 if r < RO - 1 else 96.0 * W) - SQ * SQ, A.mult, A.add, ["pA" + s, "k32"], ["sA" + rh], bank="pb" + s)
         if r < RO - 1:
-            ts(col[:, 4:5], pa, 32.0, pa, A.is_lt, A.mult, ["pA" + s], ["am" + s], bank="pm" + s)
-            act(col[:, 2:3], col[:, 4:5], F.Identity, ["am" + s, "tcol" + s], ["thr" + s], bias=col[:, 0:1])
-        ts(col[:, 3:4], pa, 32.0, K0 if r < RO - 1 else 0.0, A.mult, A.add, ["pA" + s], ["a32" + s], bank="pm" + s)
+            ts(col[:, 4:5], pa, lim, pa, A.is_lt, A.mult, ["pA" + s, "lim"], ["am" + s], bank="pb" + s)
 
     def best(r, h):
         s, rh = str(h), "%d%d" % (r, h)
         t = lambda n: T[n + s]
-        si, sm, pm, col, offs = t("si"), t("sm"), t("pm"), t("col"), t("offs")
-        b = 80 * (2 * r + h)
+        si, sm, pr, offs = t("si"), t("sm"), t("pr"), t("offs")
         kw = ["tab%sa" % s, "tab%sb" % s]
-        tt(sm[:, 144:176], t("w1")[:, 0:256].indirect(offs[:, 0:2]), sm[:, 0:32], A.mult, ["w1" + s, "offs" + s, "F0" + s, "F1" + s], ["qw" + s], ind=True)
-        tt(si[:, 16:48], sm[:, 144:176], sm[:, 96:128], A.add, ["qw" + s, "c20" + s, "c21" + s], ["ww" + s])
-        ts(si[:, 48:80], si[:, 16:48], 5, W - 1, A.arith_shift_right, A.bitwise_and, ["ww" + s], ["ew" + s])
-        cp(t("winu")[:], si[:, 48:64], ["ew" + s], ["winu" + s])
-        if XH_V:
-            op("V", lambda e: e.tensor_scalar(t("xh")[:], t("tab")[:, 0:W].indirect(t("winu")[:, 0:16]), 0.5, None, A.mult),
-               kw + ["winu" + s], ["xh" + s], 50 + 256 * CI)
-        else:
-            act(t("xh")[:], t("tab")[:, 0:W].indirect(t("winu")[:, 0:16]), F.Identity, kw + ["winu" + s], ["xh" + s], scale=0.5, ind=True)
-        cp(T.snd[:, b:b + 64:4], si[:, 48:64], ["ew" + s, "snd"], ["sL" + rh])
-        tt(sm[:, 176:192], T.rib[:, 0:256].indirect(offs[:, 0:1]), si[:, 64:80], A.mult, ["rib", "offs" + s, "ew" + s], ["tv" + s], ind=True)
-        act(sm[:, 192:224], T.hw[:, 0:256].indirect(offs[:, 0:2]), F.Identity, ["hw", "offs" + s], ["hb" + s], ind=True)
-        mm(pm[:, 96:112], T.blk32[:], sm[:, 176:192], ["blk32", "tv" + s], "pv" + s, "pm" + s, True, f32=True)
-        tt(T.snd[:, b + 11:b + 72:4], pm[:, 96:112], sm[:, 208:224], A.add, ["pv" + s, "hb" + s, "snd"], ["sP" + rh], bank="pm" + s)
-        op("V", lambda e: e.tensor_tensor_scan(t("ms")[:], T.rst[:], t("xh")[:], 0.0, A.mult, A.max), ["rst", "xh" + s], ["ms" + s], 128 * CV + FV)
+        cut = lambda n: [n + s + "a", n + s + "b"]
+        tt(sm[:, 80:96], t("w1")[:, 0:256].indirect(offs[:, 0:1]), sm[:, 16:32], A.mult, cut("w1") + ["offs" + s, "F" + s], ["qw" + s], ind=True)
+        tt(si[:, 112:128], sm[:, 80:96], sm[:, 64:80], A.add, ["qw" + s, "c32" + s], ["ww" + s])
+        ts(si[:, 128:144], si[:, 112:128], 5, W - 1, A.arith_shift_right, A.bitwise_and, ["ww" + s], ["ew" + s])
+        cp(t("winu")[:], si[:, 128:144], ["ew" + s], ["winu" + s])
+        act(t("xh")[:], t("tab")[:, 0:W].indirect(t("winu")[:, 0:16]), F.Identity, kw + ["winu" + s], ["xh" + s], scale=0.5, ind=True)
+        act(field(r, h, 0), si[:, 128:144], F.Identity, ["ew" + s], ["sL" + rh], bias=-2048.0)
+        act(sm[:, 96:112], t("e0")[:, 0:256].indirect(offs[:, 0:1]), F.Identity, cut("e0") + ["offs" + s], ["ek" + s], bias=-8192.0, ind=True)
+        tt(field(r, h, 4, pair=True), T.hwl[:, 0:256].indirect(offs[:, 2:3]), sm[:, 96:112], A.add, ["hwl", "offs" + s, "ek" + s], ["sLo" + rh], ind=True)
+        tt(field(r, h, 5, pair=True), T.hwh[:, 0:256].indirect(offs[:, 2:3]), sm[:, 96:112], A.add, ["hwh", "offs" + s, "ek" + s], ["sHi" + rh], ind=True)
+        scan(t("ms")[:], T.rst[:], t("xh")[:], A.mult, A.max, ["rst", "xh" + s], ["ms" + s])
         mh = t("ms")[:, 15:256:16]
-        tt(t("yh")[:], mh, sm[:, 32:48], A.add, ["ms" + s, "zq" + s], ["yh" + s])
-        mm(pm[:, 32:48], T.ublk[:], t("yh")[:], ["ublk", "yh" + s], "pu" + s, "pm" + s, True)
-        pd = t("pd")
-        mm(pd[:, 256:272], T.pk[:, 0:128], t("yh")[:], ["pk0", "yh" + s], "py0" + s, "pd" + s, True)
-        mm(pd[:, 272:288], T.swp[:], t("yh")[:], ["swp", "yh" + s], "py1" + s, "pd" + s, True)
-        act(t("yb")[:], pd[:, 256:288], F.Identity, ["py0" + s, "py1" + s], ["yb" + s], bias=-YOFF, bank="pd" + s)
-        tt(sm[:, 224:240], sm[:, 32:48], mh, A.subtract, ["ms" + s, "zq" + s], ["dz" + s])
-        act(T.snd[:, b + 1:b + 64:4], sm[:, 224:240], F.Abs, ["dz" + s, "snd"], ["sZ" + rh], bias=0.5 - 2 * YOFF, scale=2.0)
-        cp(si[:, 80:96], pm[:, 32:48], ["pu" + s], ["ui" + s], bank="pm" + s)
-        ts(si[:, 96:112], si[:, 80:96], W - 1, None, A.bitwise_and, None, ["ui" + s], ["u" + s])
-        tt(si[:, 112:128], si[:, 96:112], si[:, 96:112], A.mult, ["u" + s], ["sq" + s])
-        ts(si[:, 128:144], si[:, 112:128], 32 * W - 32, None, A.bitwise_and, None, ["sq" + s], ["s" + s])
-        ts(sm[:, 240:256], si[:, 96:112], 1184.0, col[:, 3:4], A.mult, A.add, ["u" + s, "a32" + s], ["r" + s])
-        out = T.snd[:, b + 2:b + 64:4]
-        if r < RO - 1:
-            tt(out, si[:, 128:144], sm[:, 240:256], A.add, ["s" + s, "r" + s, "snd"], ["sC" + rh])
-        else:
-            tt(si[:, 144:160], si[:, 128:144], sm[:, 240:256], A.add, ["s" + s, "r" + s], ["c1" + s])
-            ts(si[:, 160:176], si[:, 144:160], 5, W - 1, A.arith_shift_right, A.bitwise_and, ["c1" + s], ["c2" + s])
-            cp(out, si[:, 160:176], ["c2" + s, "snd"], ["sC" + rh])
-        exchange(r, h, ["sL" + rh, "sZ" + rh, "sC" + rh, "sP" + rh])
-        for l in range(16):
-            mm(pd[:, 288:290], T.uw[:, 15 - l:143 - l], t("yb")[:, l:32:16], ["uw", "yb" + s], "pt" + s, "pd" + s, l == 0)
-        cp(si[:, 4:6], pd[:, 288:290], ["pt" + s], ["pli" + s], bank="pd" + s)
-        ts(si[:, 6:8], si[:, 4:6], 127, None, A.bitwise_and, None, ["pli" + s], ["plj" + s])
+        cp(field(r, h, 1), mh, ["ms" + s], ["sM" + rh])
+        exchange(r, h)
+        yh = t("yh")[:, 16:32]
+        tt(yh, mh, field(r, h, 2), A.add, ["ms" + s, "sQ" + rh], ["yh" + s])
         for c in range(2):
-            ts(t("plu")[:, c:c + 1], si[:, 6 + c:7 + c], cf[:, 12 + c:13 + c], None, A.add, None, ["plj" + s, "pb%d" % c], ["plu%d%s" % (c, s)])
+            mm(pr[:, 256 + 16 * c:272 + 16 * c], T.pick[:, 128 * c:128 * c + 128], yh, ["pick", "yh" + s], "py%d%s" % (c, s), "pr" + s, True)
+        act(t("yb")[:], pr[:, 256:288], F.Identity, ["py0" + s, "py1" + s], ["yb" + s], bias=-YOFF, bank="pr" + s)
+        for l in range(16):
+            mm(pr[:, 288:290], T.uw[:, 15 - l:143 - l], t("yb")[:, l:32:16], ["uw", "yb" + s], "pt" + s, "pr" + s, l == 0)
+        act(si[:, 144:146], pr[:, 288:290], F.Identity, ["pt" + s], ["pli" + s], bank="pr" + s)
+        ts(si[:, 146:148], si[:, 144:146], 127, None, A.bitwise_and, None, ["pli" + s], ["plj" + s])
+        for c in range(2):
+            act(t("plu")[:, c:c + 1], si[:, 146 + c:147 + c], F.Identity, ["plj" + s, "lbase%d" % c], ["plu%d%s" % (c, s)], bias=cf[:, 17 + c:18 + c])
         cp(t("tab")[:, 0:W].indirect(t("plu")[:, 0:2]), t("yb")[:], ["plu0" + s, "plu1" + s, "yb" + s], kw, c=180.0)
         if r == RO - 1:
-            dma("Y", T.yx[64 * h:64 * h + 64, :], t("tab")[0:64, :], kw, ["yx" + s], "d_yx" + s, LAT_DMA + 1800)
+            dma("Y", T.yx[64 * h:64 * h + 64, :], t("tab")[0:64, :], kw + ["s" + rh], ["yx" + s], "d_yx" + s, LAT_DMA + 1800)
 
     def leave(h):
-        s, b = str(h), 80 * (2 * (RO - 1) + h)
+        s = str(h)
         t = lambda n: T[n + s]
-        key, ot, lof, pm = "rcv%d%d" % (RO - 1, h), t("ot"), T.lof[:, 0:1], t("pm")
-        lists(RO - 1, h)
-        cp(ot[:, 32:64].indirect(lof), T.rcv[:, b + 2:b + 64:4], [key, "lof"], ["ot1" + s], c=110.0)
-        cp(ot[:, 64:96].indirect(lof), T.rcv[:, b + 1:b + 64:4], [key, "lof"], ["ot2" + s], c=110.0)
-        cp(ot[:, 0:32].indirect(lof), t("li")[:], ["li" + s, "lof"], ["ot0" + s], c=110.0)
-        mm(pm[0:64, 96:160], T.mrg[:], ot[:, 32:96], ["mrg", "ot1" + s, "ot2" + s], "po1" + s, "pm" + s, True, f32=True)
-        act(t("oz")[0:64, :], pm[0:64, 128:160], F.Identity, ["po1" + s], ["oz" + s], bank="pm" + s)
-        act(t("of")[0:64, 32:64], pm[0:64, 96:128], F.Identity, ["po1" + s], ["oc" + s], bank="pm" + s)
-        pz = t("pzl")
-        mm(pz[0:64, 0:32], T.mrg[:], ot[:, 0:32], ["mrg", "ot0" + s], "pzl%s_0" % s, "pzl" + s, True, f32=True)
-        cp(t("of")[0:64, 0:32], pz[0:64, 0:32], ["pzl%s_0" % s], ["ol" + s], bank="pzl" + s)
+        si, zl, pr, pb = t("si"), t("zl"), t("pr"), t("pb")
+        arrive(RO - 1, h)
+        act(t("zt")[:], field(RO - 1, h, 3, True), F.Identity, ["rcv%d%d" % (RO - 1, h)], ["zt" + s])
+        ka = unfold(pb, T.pick, 128, t("zt"), 16, ["pick", "zt" + s], "oa" + s, "pb" + s)
+        tt(si[0:64, 64:96], si[0:64, 152:184], pb[0:64, 0:32], A.add, ["sq" + s] + ka, ["key" + s], bank="pb" + s)
+        ts(si[0:64, 112:144], si[0:64, 64:96], 5, W - 1, A.arith_shift_right, A.bitwise_and, ["key" + s], ["ww" + s, "ew" + s])
+        cp(t("of")[0:64, 32:64], si[0:64, 112:144], ["ww" + s], ["oc" + s])
+        ko = unfold(pr, T.pick, 128, zl, 32, ["pick", "zl" + s, "z" + s], "ol" + s, "pr" + s)
+        act(t("of")[0:64, 0:32], pr[0:64, 0:32], F.Identity, ko, ["ol" + s], bias=2048.0, bank="pr" + s)
+        act(t("oz")[0:64, :], pr[0:64, 32:64], F.Identity, ko, ["oz" + s], bank="pr" + s)
         dma("S", T.yz[64 * h:64 * h + 64, :], t("oz")[0:64, :], ["oz" + s], ["yz" + s], "d_yz" + s, LAT_DMA)
-        dma("S", T.ya[4 * h:4 * h + 4, :], t("of")[0:64:16, 32:64], ["oc" + s], ["ya" + s], "d_ya" + s, LAT_DMA)
+        dma("Y", T.ya[4 * h:4 * h + 4, :], t("of")[0:64:16, 32:64], ["oc" + s], ["ya" + s], "d_ya" + s, LAT_DMA)
         dma("Y", T.yl[64 * h:64 * h + 64, :], t("of")[0:64, 0:32], ["ol" + s], ["yl" + s], "d_yl" + s, LAT_DMA)
 
-    prep(0, 0)
-    prep(0, 1)
     for r in range(RO):
         for h in range(2):
+            prep(r, h)
             gath(r, h)
-            if h == 0 and r > 0:
-                prep(r, 1)
             counts(r, h)
             best(r, h)
-            if h == 1 and r < RO - 1:
-                prep(r + 1, 0)
     leave(0)
     leave(1)
-    return ops, groups, sent[0]
+    return ops, groups
 
 
 def plan(ops):
@@ -478,7 +499,7 @@ def plan(ops):
 
     def replay(order, case):
         cost, lat, pred, _ = case
-        free, st = {e: 0.0 for e in "VSPGY"}, [0.0] * n
+        free, st = {e: 0.0 for e in "VSPGYZ"}, [0.0] * n
         for k in order:
             st[k] = max([st[j] + cost[j] + gap for j, gap in pred[k]] + [free[ops[k]["eng"]]])
             free[ops[k]["eng"]] = st[k] + cost[k]
@@ -486,7 +507,7 @@ def plan(ops):
 
     def place(seq, back, cost, slack, case):
         _, lat, pred, succ = case
-        busy = {e: [] for e in "VSPGY"}
+        busy = {e: [] for e in "VSPGYZ"}
         st = [0.0] * n
         for k in seq:
             c = cost[k]
@@ -527,13 +548,14 @@ def rank_program(g, core, T, topo):
     rank = T.rank_of(core)
     if rank is None:
         return
-    ops, groups, sent = build(T, topo, rank)
+    ops, groups = build(T, topo, rank)
     if "order" not in PLAN:
         PLAN["order"] = plan(ops)[0]
     order = PLAN["order"]
     at = {k: j for j, k in enumerate(order)}
     last = set(max(gr, key=lambda k: at[k]) for gr in groups)
     queue = {"V": g.vector, "S": g.scalar, "P": g.tensor, "G": g, "Y": g.sync}
+    order = [k for k in order if ops[k]["fn"] is not None]
     known = {e: {} for e in queue}
     snap, waits, marked = {}, {}, set()
     for k in order:
@@ -551,9 +573,10 @@ def rank_program(g, core, T, topo):
             if p["sem"] is None:
                 marked.add(d)
             kn[key] = at[d]
-            for x, v in snap[d].items():
-                if kn.get(x, -1) < v:
-                    kn[x] = v
+            if p["sem"] is None or p["sem"][0].startswith("d_"):
+                for x, v in snap[d].items():
+                    if kn.get(x, -1) < v:
+                        kn[x] = v
         waits[k] = ws
         snap[k] = dict(kn)
     count, tick = {e: 0 for e in queue}, {}
@@ -578,4 +601,6 @@ def rank_program(g, core, T, topo):
     for n in ("yx", "yl", "yz", "ya"):
         for h in range(2):
             g.sync.wait_ge(T.sem["d_%s%d" % (n, h)], 16)
-    g.wait_ge(T.sem.sent, sent)
+    for r in range(RO):
+        for h in range(2):
+            g.wait_ge(T.sem["s%d%d" % (r, h)], len(HOPS))

import numpy as np
from concourse.bass import DstId, RemoteDMATransfer
from concourse.mybir import AluOpType, AxisListType, ActivationFunctionType

N, W, LN, RO, BL = 8, 4096, 32, 3, 4
DIST = [1 + (l // BL) % (N - 1) for l in range(LN)]
HOPS = [DIST[BL * b] for b in range(LN // BL)] + [DIST[LN - 1] + 1]
NF = 6
SLOT = 2 * NF
SET = SLOT * len(HOPS)
RUN = 17
WALKS = ((0, 12, 2), (12, 16, 4))
SPLIT = ()
ZW = 16 * (16 + len(WALKS))
ZP = [0, 16 * (WALKS[0][1] + 1) * WALKS[0][2]]
ZP.append(ZP[1] + 16 * (17 - WALKS[1][0]) * WALKS[1][2])
ON_V = (0, 2, 4, 6, 9)
FINE = [(r, h) for r in range(RO) for h in range(2)]
EARLY = [(r, h) for r in range(RO) for h in range(2)]
YOFF = 1536.0
SQ = 592

SCRATCH = {
    "at8": ("sbuf", [128, 40], "int32"), "af8": ("sbuf", [128, 40], "float16"),
    "ci": ("sbuf", [128, 8], "int32"), "cf": ("sbuf", [128, 24], "float32"),
    "tci": ("sbuf", [128, 16], "int32"), "tcf": ("sbuf", [128, 16], "float32"), "diag": ("sbuf", [128, 16], "float32"),
    "k32": ("sbuf", [128, 16], "float32"), "lof": ("sbuf", [128, 8], "uint16"), "rep": ("sbuf", [128, 16], "uint16"),
    "msg": ("sbuf", [128, 4 * RO * SET], "float32"),
}
for _n, _s in (("iob", 144), ("pk", 2048), ("pi", 2048), ("pick", 256), ("blk", 128), ("blk2", 128), ("ublk", 128), ("bw1", 144), ("uw", 144),
               ("par", 1024), ("b9", 8 * RUN), ("wx", 8 * RUN), ("wm", 8 * RUN), ("sp", 8 * RUN + ZW), ("sa", 8 * RUN + ZW), ("sb", 8 * RUN + ZW),
               ("r2", 32), ("kp", 32), ("rst", 256), ("sel", 256),
               ("hwl", 256), ("hwh", 256), ("one", 128), ("c20", 256)):
    SCRATCH[_n] = ("sbuf", [128, _s], "bfloat16")
for _h in "01":
    for _n, _s, _d in (("tab", W, "bfloat16"), ("lsb", 32, "int32"), ("zsb", 32, "bfloat16"),
                       ("cin", 32, "float32"), ("col", 8, "float32"), ("hot", 2, "bfloat16"), ("yb", 32, "bfloat16"),
                       ("plu", 2, "uint16"), ("of", 64, "float32"), ("oz", 32, "bfloat16"), ("zl", 48, "float16"),
                       ("w1", 256, "float32"), ("q", 256, "float32"), ("wi", 256, "int32"), ("e0", 256, "int32"), ("eu", 256, "uint16"),
                       ("gg", 16 * ZW, "bfloat16"), ("mn", 16 * ZW, "bfloat16"), ("mask", 256, "bfloat16"),
                       ("zs", 16, "bfloat16"), ("zt", 16, "float16"), ("zp", ZP[2], "bfloat16"),
                       ("sm", 112, "float32"), ("si", 184, "int32"), ("offs", 4, "uint16"), ("winu", 16, "uint16"),
                       ("xh", 256, "bfloat16"), ("ms", 256, "bfloat16"), ("yh", 32, "float16")):
        SCRATCH[_n + _h] = ("sbuf", [128, _s], _d)
    for _n in ("pr", "pb", "pd", "pz"):
        SCRATCH[_n + _h] = ("psum", [128, 512], "float32")

SEMAPHORES = (["eV", "eS", "eP", "eG", "d_an", "d_th"]
              + ["d_%s%d" % (n, h) for n in ("xa", "xb", "la", "lb", "za", "zb", "yx", "yl", "ya", "yz") for h in range(2)]
              + [n + "%d%d" % (r, h) for n in "as" for r in range(RO) for h in range(2)])

A = AluOpType
F = ActivationFunctionType
X = AxisListType.X
CASES = np.array([[1.04, 0.92, 1.20, 1.00], [1.60, 1.20, 2.20, 1.35], [0.52, 0.46, 0.60, 0.52], [20.0, 20.0, 30.0, 50.0], [30.0, 30.0, 60.0, 60.0],
                  [70.0, 150.0, 100.0, 60.0], [130.0, 220.0, 200.0, 100.0], [2000.0, 2000.0, 2500.0, 1500.0], [3000.0, 2500.0, 5000.0, 3500.0]])
CV, CI, CP, FV, FS, LAT_SAME, LAT_X, LAT_DMA, LAT_REM = CASES
PASSES, TRIES, FRESH = 4, 120, 40
PLAN = {}


def level(j):
    return 2.0 ** (8 * j - 64)


def engine_split(topo, src, dsts):
    out = {}
    for j in sorted(range(len(dsts)), key=lambda j: len(topo.engines(src, dsts[j]))):
        free = [e for e in topo.engines(src, dsts[j]) if e not in out.values()]
        out[j] = free[0] if topo.chip(dsts[j]) != topo.chip(src) else free[-1]
    return out


def build(T, topo, rank):
    ops, res, banks, groups = [], {}, {}, []

    def op(eng, fn, r, w, cost, bank=None, sem=None, acc=None, lat=0.0):
        k = len(ops)
        deps = set()
        for x in r:
            s = res.setdefault(x, [[], []])
            deps.update(s[0])
            s[1].append(k)
        for x in w:
            s = res.setdefault(x, [[], []])
            deps.update(s[0])
            deps.update(s[1])
            res[x] = [[k], []]
        if acc is not None:
            s = res[acc]
            deps.add(s[0][0])
            s[0].append(k)
        if bank is not None:
            b = banks.setdefault(bank, [None, [], []])
            if b[0] != eng:
                b[0], b[2], b[1] = eng, b[1], []
            deps.update(b[2])
            b[1].append(k)
        deps.discard(k)
        ops.append({"eng": eng, "fn": fn, "deps": deps, "cost": cost, "sem": sem, "lat": lat, "name": (list(w) + [acc])[0]})
        return k

    def n_of(ap):
        n = 1
        for s in ap.shape[1:]:
            n *= s
        return n

    def ts(out, in0, s1, s2, o0, o1, r, w, bank=None, half=False, ind=False):
        c = 50 + n_of(out) * CI if ind else max(64, n_of(out) * (0.5 if half else 1)) * CV + FV
        if o1 is None:
            return op("V", lambda e: e.tensor_scalar(out, in0, s1, None, o0), r, w, c, bank)
        return op("V", lambda e: e.tensor_scalar(out, in0, s1, s2, o0, o1), r, w, c, bank)

    def tt(out, a, b, o, r, w, bank=None, ind=False):
        n = n_of(out)
        c = 50 + n * CI if ind else max(64, n * (1 if bank else 2)) * CV + FV
        return op("V", lambda e: e.tensor_tensor(out, a, b, o), r, w, c, bank)

    def cp(out, a, r, w, bank=None, c=None):
        return op("V", lambda e: e.tensor_copy(out, a), r, w, c or max(64, n_of(out)) * CV + FV, bank)

    def scan(out, a, b, o0, o1, r, w, bank=None):
        c = max(64, n_of(out) * (1 if bank else 0.5)) * CV + FV
        return op("V", lambda e: e.tensor_tensor_scan(out, a, b, 0.0, o0, o1), r, w, c, bank)

    def act(out, a, f, r, w, bias=0.0, scale=1.0, bank=None, ind=False):
        n = n_of(out)
        c = 65 + n * CI if ind else max(64, n) * CV + FS
        return op("S", lambda e: e.activation(out, a, f, bias, scale), r, w, c, bank)

    def gcp(out, a, r, w):
        return op("G", lambda e: e.affine_select(out, a, [[0, n_of(out)]], A.is_ge, 0.0, 0, 0), r, w, 170 + 2 * n_of(out) * CV)

    def fill(ap, v, w):
        return iota(ap, [[0, n_of(ap)]], int(v), 0, w)

    def mm(out, lt, rh, r, key, bank, first, f32=False):
        c = max(64, n_of(out)) * CP * (4 if f32 else 1)
        fn = lambda e, stop: e.matmul(out, lt, rh, first, stop)
        if first:
            k = op("P", fn, r, [key], c, bank)
            groups.append([k])
            res[key].append(len(groups) - 1)
        else:
            k = op("P", fn, r, [], c, bank, acc=key)
            groups[res[key][2]].append(k)
        return k

    def iota(out, pat, base, cm, w, whole=False):
        if whole:
            return op("G", lambda e: e.iota(out, pat, base, cm), [], w, 130 + 2 * CV * n_of(out))
        return op("G", lambda e: e.iota(out, pat, base, cm, allow_small_or_imprecise_dtypes=True), [], w, 130 + 2 * CV * n_of(out))

    def dma(q, out, a, r, w, sem, lat):
        return op(q, lambda e: e.dma_start(out, a), r, w, 100.0, sem=(sem, 16), lat=lat)

    def base(r, h):
        return 2 * SET * (2 * r + h)

    def field(r, h, f, came=False, pair=False, lo=0, hi=16):
        b = base(r, h) + (SET if came else 0) + (SLOT if pair else 0) + f
        return T.msg[:, b + lo * NF:b + (hi - 1) * NF + 1:NF]

    def sent_keys(r, h):
        return [n + "%d%d" % (r, h) for n in ("sL", "sM", "sQ", "sA", "sLo", "sHi")]

    def exchange(r, h):
        b, name, me = base(r, h), "a%d%d" % (r, h), T.cores[rank]
        dst = [T.cores[(rank + d) % N] for d in HOPS]
        sp = engine_split(topo, me, dst)
        trs, left = [], "s%d%d" % (r, h)
        for j, d in enumerate(dst):
            rid, pid, _ = topo.addr(d)
            a = b + SLOT * j
            trs.append(RemoteDMATransfer(dst_ids=[DstId(rid=rid, pnc=pid)], dma_engine_mask=1 << sp[j], remote_sem=T.sem[name],
                                         src=T.msg[:, a:a + SLOT], dst=T.msg[:, a + SET:a + SET + SLOT]))
        wait = ["yx0"] if (r, h) == (RO - 1, 1) else []
        k = op("G", lambda e: e.remote_dma_fused(trs, local_sem=T.sem[left]), sent_keys(r, h) + wait, ["rcv%d%d" % (r, h)], 1000.0,
               sem=(name, len(HOPS)), lat=LAT_REM)
        ops[op("Z", None, [], [left], 0.0, sem=(left, len(HOPS)), lat=LAT_REM - 1000)]["after"] = k

    dma("S", T.at8[0:8, 0:32], T.an[:], [], ["an"], "d_an", LAT_DMA)
    dma("S", T.at8[0:8, 32:33], T.th[:], [], ["th"], "d_th", LAT_DMA)
    prev = None
    for h in range(2):
        s = str(h)
        for n, src, buf, q, lat in (("l", T.ls, "lsb", "Y", LAT_DMA), ("z", T.z, "zsb", "S", LAT_DMA), ("x", T.x, "tab", "Y", LAT_DMA + 3500)):
            for c in range(2):
                wait = ["tab0a", "tab0b"] if (n, h) == ("x", 1) else []
                k = dma(q, T[buf + s][64 * c:64 * c + 64, :], src[64 * h:64 * h + 64, :], wait, [buf + s + "ab"[c]], "d_" + n + "ab"[c] + s, lat)
                if q == "Y":
                    if prev is not None:
                        ops[k]["after"] = prev
                    prev = k

    cf = T.cf
    c2col, gcol, fcol, g4col, ocol, last2, pcol = [cf[:, j:j + 1] for j in range(1, 8)]
    g15, wcol, l2, top, lim, ndel, nb2, lo = [cf[:, j:j + 1] for j in range(8, 16)]
    iota(T.ci[:, 7:8], [[0, 1]], 0, 1, ["p"], True)
    iota(T.tci[:], [[-1, 16]], 16, 1, ["tci"], True)
    iota(T.iob[:], [[1, 144]], 0, 0, ["iob"])
    iota(T.blk[:], [[16, 8], [0, 16]], 0, 0, ["blk"])
    for h in range(2):
        iota(T.sel[0:8, 128 * h:128 * h + 128], [[0, 2], [1, 4], [0, 16]], 4 * h, -1, ["sel%d" % h])
    iota(T.sa[:, 0:8 * RUN], [[0, 8], [1, RUN]], 0, 0, ["sa0"])
    for x, (a, b, _) in enumerate(WALKS):
        iota(T.sa[:, 8 * RUN + 16 * (a + x):8 * RUN + 16 * (b + x + 1)], [[0, 16], [1, b - a + 1]], 0, 0, ["sa%d" % (x + 1)])
    fill(T.one[:], 1, ["one"])
    fill(T.c20[0:1, :], 2080, ["c20"])
    iota(T.b9[:], [[16, 8], [0, RUN]], 0, 0, ["b9"])
    iota(T.kp[0:1, :], [[0, 2], [-1, 16]], 143, 0, ["kp"])
    iota(T.hwl[:], [[0, 16], [1, 16]], 0, 0, ["hwl"])
    iota(T.blk2[:], [[0, 2], [16, 4], [0, 16]], 0, 0, ["blk2"])
    iota(T.pick[:], [[64, 2], [0, 2], [1, 64]], 0, 0, ["pick"])
    fill(T.k32[:], 32, ["k32"])
    p = T.ci[:, 7:8]
    for j, m in ((2, 0x70), (3, 15), (4, 0x30), (5, 1), (6, 14)):
        ts(T.ci[:, j:j + 1], p, m, None, A.bitwise_and, None, ["p"], ["p%d" % j])
    ts(T.ci[:, 1:2], p, 5, 2, A.arith_shift_right, A.bitwise_and, ["p"], ["p1"])
    cp(cf[:, 1:8], T.ci[:, 1:8], ["p"] + ["p%d" % j for j in range(1, 7)], ["cf"])
    ts(T.tci[:], T.tci[:], 15, None, A.bitwise_and, None, ["tci"], ["tci"])
    ts(T.tcf[:], T.tci[:], gcol, None, A.add, None, ["tci", "cf"], ["tcf"])
    ts(T.blk[:], T.blk[:], gcol, None, A.is_equal, None, ["blk", "cf"], ["blk"], half=True)
    ts(T.diag[:], T.iob[:, 0:16], fcol, None, A.is_equal, None, ["iob", "cf"], ["diag"])
    for k in range(16):
        ts(T.pk[:, 128 * k:128 * k + 128], T.iob[:, 0:128], T.tcf[:, k:k + 1], None, A.is_equal, None, ["iob", "tcf"], ["pk%d" % k], half=True)
        if k % 2:
            ts(T.pi[:, 128 * k:128 * k + 128], T.blk[:], T.diag[:, k:k + 1], None, A.mult, None, ["blk", "diag"], ["pi%d" % k], half=True)
        else:
            act(T.pi[:, 128 * k:128 * k + 128], T.blk[:], F.Identity, ["blk", "diag"], ["pi%d" % k], scale=T.diag[:, k:k + 1])
    act(l2, last2, F.Identity, ["cf"], ["l2"], bias=ocol, scale=2.0)
    ts(T.lof[:, 0:1], l2, c2col, None, A.add, None, ["cf", "l2"], ["lof"])
    for c in range(2):
        act(cf[:, 17 + c:18 + c], l2, F.Identity, ["l2"], ["lbase%d" % c], bias=256.0 * c, scale=128.0)
    cp(T.rep[:], T.iob[:, 0:16], ["iob"], ["rep"])
    act(g15, gcol, F.Identity, ["cf"], ["g15"], bias=15.0)
    act(wcol, fcol, F.Identity, ["cf"], ["wcol"], bias=1.0, scale=2.0)
    act(top, fcol, F.Identity, ["cf"], ["top"], bias=15.0, scale=16.0)
    act(lim, T.diag[:, 0:1], F.Identity, ["diag"], ["lim"], bias=-1.0, scale=33.0)
    act(ndel, T.diag[:, 0:1], F.Identity, ["diag"], ["ndel"], scale=-1.0)
    act(nb2, T.diag[:, 0:1], F.Identity, ["diag"], ["nb2"], bias=-127.0, scale=0.5)
    home = [2 * b for b in range(LN // BL) if (DIST[BL * b] + 1) % N == 0][0]
    ts(lo, last2, float(home), -float(SET), A.is_equal, A.mult, ["cf"], ["lo0"])
    act(lo, fcol, F.Identity, ["lo0", "cf"], ["lo0"], bias=lo, scale=float(NF))
    ts(T.lof[:, 2:3], lo, float(SET + SLOT + 5), None, A.add, None, ["lo0"], ["lof1"])
    a = 8 * RUN + 16 * (WALKS[0][1] + 1)
    ts(T.sb[:, 0:a], T.sa[:, 0:a], 0.0, level(-1), A.is_equal, A.mult, ["sa0", "sa1"], ["sb0"], half=True)
    ts(T.sb[:, a:], T.sa[:, a:], 0.0, level(WALKS[1][0] - 1), A.is_equal, A.mult, ["sa2"], ["sb1"], half=True)
    ts(T.sa[:], T.sa[:], 0.0, 256.0, A.is_gt, A.mult, [], ["sa0", "sa1", "sa2"], half=True)
    scan(T.sp[:], T.sa[:], T.sb[:], A.mult, A.max, ["sa0", "sb0", "sb1"], ["sp"])
    ts(T.b9[:], T.b9[:], gcol, 256.0, A.is_equal, A.mult, ["b9", "cf"], ["b9"], half=True)
    tt(T.wx[:], T.b9[:], T.sp[:, 0:8 * RUN], A.mult, ["b9", "sp"], ["wx"])
    act(T.wm[:], T.wx[:], F.Identity, ["wx"], ["wm"], scale=-2.0)
    for g in range(8):
        ts(T.par[:, 128 * g:128 * g + 128], T.one[:], T.blk[:, 16 * g:16 * g + 1], None, A.mult, None, ["one", "blk"], ["par%d" % g], half=True)
    act(T.r2[:, 0:16], T.diag[:], F.Identity, ["diag"], ["r2a"], scale=8.0)
    act(T.r2[:, 16:32], T.diag[:], F.Identity, ["diag"], ["r2b"], scale=-8.0)
    ts(T.rst[:], T.hwl[:], 0.0, None, A.is_gt, None, ["hwl"], ["rst"], half=True)
    ts(T.hwl[:], T.hwl[:], fcol, 6144.0, A.is_equal, A.mult, ["hwl", "cf"], ["hwl"], half=True)
    ts(T.hwh[:], T.hwl[:], -1.0, 12288.0, A.mult, A.add, ["hwl"], ["hwh"], half=True)
    ts(T.blk2[:], T.blk2[:], g4col, 0.5, A.is_equal, A.mult, ["blk2", "cf"], ["blk2"], half=True)
    ts(T.pick[:], T.pick[:], pcol, None, A.is_equal, None, ["pick", "cf"], ["pick"], half=True)
    ts(T.bw1[:], T.iob[:], g15, None, A.is_equal, None, ["iob", "g15"], ["bw1"], half=True)
    act(T.uw[:], T.bw1[:], F.Identity, ["bw1", "wcol"], ["uw"], scale=wcol)
    ts(T.ublk[:], T.blk[:], wcol, None, A.mult, None, ["blk", "wcol"], ["ublk"], half=True)
    act(T.af8[0:8, 0:33], T.at8[0:8, 0:33], F.Identity, ["an", "th"], ["af8"], bias=-2048.0)
    for h in range(2):
        s = str(h)
        sel = T.sel[0:8, 128 * h:128 * h + 128]
        ts(sel, sel, 0.0, None, A.is_equal, None, ["sel" + s], ["sel" + s], half=True)
        px = T["pz" + s]
        mm(px[:, 0:33], sel, T.af8[0:8, 0:33], ["sel" + s, "af8"], "px" + s, "pz" + s, True)
        act(T["cin" + s][:], px[:, 0:32], F.Identity, ["px" + s], ["cin" + s], bias=32.0 * (32 - 2048), scale=32.0, bank="pz" + s)
        act(T["col" + s][:, 0:1], px[:, 32:33], F.Identity, ["px" + s, "ndel", "nb2"], ["nb0" + s], bias=nb2, scale=ndel, bank="pz" + s)
        for x, (lo_, hi, rep) in enumerate(WALKS):
            fill(T["gg" + s][:, 256 * (lo_ + x):256 * (hi + x + 1):hi - lo_ + 1], 0, ["gz%s%d" % (s, x)])
    for r in range(RO):
        for h in range(2):
            fill(T.msg[:, base(r, h):base(r, h) + SET], 0, sent_keys(r, h))

    def unfold(out, lt, step, src, n, r, key, bank):
        keys = []
        for c in range(2):
            for u in range(2):
                keys.append("%s_%d%d" % (key, c, u))
                mm(out[0:64, 2 * c + u:2 * n:4], lt[:, step * c:step * c + 64], src[:, u:n:2], r, keys[-1], bank, True)
        return keys

    def arrive(r, h):
        s, rh = str(h), "%d%d" % (r, h)
        t = lambda n: T[n + s]
        sm, si, key = t("sm"), t("si"), "rcv" + rh
        win = T.msg[:, base(r, h):base(r, h) + 2 * SET]
        kw = [key] + sent_keys(r, h)
        for a, b in ((0, home), (home, home + 2), (home + 2, 16)):
            tt(sm[:, a:b], field(r, h, 0, True, False, a, b), field(r, h, 4, a != home, True, a, b), A.max, kw, ["m%d%s" % (a, s)])
        tt(t("zl")[:, 0:16], win.indirect(T.lof[:, 2:3]), sm[:, 0:16], A.min, kw + ["lof1"] + ["m%d%s" % (a, s) for a in (0, home, home + 2)],
           ["zl" + s], ind=True)
        mh, zq = field(r, h, 1, True), field(r, h, 2, True)
        tt(t("yh")[:, 0:16], mh, zq, A.add, [key], ["yr" + s])
        if r < RO - 1:
            p, n, keys = 128, 16, ["pu" + s]
            mm(t("pd")[:, 0:16], T.ublk[:], t("yh")[:, 0:16], ["ublk", "yr" + s], "pu" + s, "pd" + s, True)
        else:
            p, n = 64, 32
            keys = unfold(t("pd"), T.ublk, 64, t("yh"), 16, ["ublk", "yr" + s], "pu" + s, "pd" + s)
        act(si[0:p, 0:n], t("pd")[0:p, 0:n], F.Identity, keys, ["ui" + s], bank="pd" + s)
        ts(si[0:p, 32:32 + n], si[0:p, 0:n], W - 1, None, A.bitwise_and, None, ["ui" + s], ["u" + s])
        act(si[0:p, 152:152 + n], si[0:p, 32:32 + n], F.Square, ["u" + s], ["sq" + s], bias=float(SQ))
        tt(sm[:, 48:64], zq, mh, A.subtract, [key], ["dz" + s])
        z = sm[:, 32:48] if r < RO - 1 else t("zl")[:, 16:32]
        act(z, sm[:, 48:64], F.Abs, ["dz" + s], ["z" + s], bias=0.5 - 2 * YOFF, scale=2.0)

    def prep(r, h):
        s, rh = str(h), "%d%d" % (r, h)
        t = lambda n: T[n + s]
        sm, si, zl, col = t("sm"), t("si"), t("zl")[:, 0:16], t("col")
        z, c32 = sm[:, 32:48], sm[:, 64:80]
        if r == 0:
            lof = T.lof[:, 0:1]
            ts(zl, t("lsb")[:, 0:32].indirect(lof), -2048.0, None, A.add, None, ["lsb%sa" % s, "lsb%sb" % s, "lof"], ["zl" + s], ind=True)
            act(z, t("zsb")[:, 0:32].indirect(lof), F.Identity, ["zsb%sa" % s, "zsb%sb" % s, "lof"], ["z" + s], ind=True)
            act(c32, t("cin")[:, 0:32].indirect(lof), F.Identity, ["cin" + s, "lof"], ["c32" + s], ind=True)
            act(t("zt")[:], z, F.Identity, ["z" + s, "nb0" + s], ["zt" + s], bias=col[:, 0:1])
        else:
            arrive(r - 1, h)
            ts(si[:, 48:64], si[:, 152:168], 32 * W - 32, None, A.bitwise_and, None, ["sq" + s], ["s" + s])
            tt(c32, si[:, 48:64], field(r - 1, h, 3, True), A.add, ["s" + s, "rcv%d%d" % (r - 1, h)], ["c32" + s])
            ts(t("zt")[:], z, col[:, 4:5], col[:, 0:1], A.subtract, A.add, ["z" + s, "am" + s, "nb0" + s], ["zt" + s])
        pr, pb, pz = t("pr"), t("pb"), t("pz")
        mm(pb[:, 0:256], T.one[0:1, :], T.c20[0:1, :], ["one", "c20"], "li" + s, "pb" + s, True)
        for i in range(16):
            mm(pr[:, i:256:16], T.pk[:, 128 * i:128 * i + 128], zl, ["pk%d" % i, "zl" + s], "la%s_%d" % (s, i), "pr" + s, True)
        for i in range(16):
            mm(pb[:, i:256:16], T.pi[:, 128 * i:128 * i + 128], zl, ["pi%d" % i, "zl" + s], "li" + s, "pb" + s, False)
        cuts = ((0, 64, "a"), (64, 256, "b")) if (r, h) in EARLY else ((0, 256, "ab"),)
        kc = lambda n, c: [n + s + x for x in c]
        for a, b, c in cuts:
            act(t("w1")[:, a:b], pr[:, a:b], F.Identity, ["la%s_%d" % (s, i) for i in range(16)], kc("w1", c), bias=2016.0, bank="pr" + s)
        for a, b, c in cuts:
            tt(t("q")[:, a:b], pb[:, a:b], t("w1")[:, a:b], A.mult, ["li" + s] + kc("w1", c), kc("q", c), bank="pb" + s)
        for a, b, c in cuts:
            tt(t("wi")[:, a:b], c32.indirect(T.rep[:, a // 16:b // 16]), t("q")[:, a:b], A.add, kc("q", c) + ["c32" + s, "rep"], kc("wi", c), ind=True)
            ts(t("e0")[:, a:b], t("wi")[:, a:b], 5, W - 1, A.arith_shift_right, A.bitwise_and, kc("wi", c), kc("e0", c))
            cp(t("eu")[:, a:b], t("e0")[:, a:b], kc("e0", c), kc("eu", c))
        act(sm[:, 16:32], zl, F.Identity, ["zl" + s], ["F" + s], bias=2080.0)
        act(field(r, h, 2), z, F.Identity, ["z" + s], ["sQ" + rh], bias=YOFF - 0.25, scale=0.5)
        tt(t("zs")[:], z, T.sp[:, 1:RUN], A.mult, ["z" + s, "sp"], ["zs" + s])
        mm(pz[:, 0:ZW], T.one[0:1, :], T.sp[0:1, 8 * RUN:8 * RUN + ZW], ["one", "sp"], "pz" + s, "pz" + s, True)
        for x, (lo, hi, rep) in enumerate(WALKS):
            for k in range(16):
                a = 16 * (lo + x) + (hi - lo + 1) * k + 1
                mm(pz[:, a:a + hi - lo], T.pk[:, 128 * k:128 * k + 128], t("zs")[:, lo:hi], ["pk%d" % k, "zs" + s], "pz" + s, "pz" + s, False)
        a = ZP[1] - 16 * (WALKS[0][1] + 1)
        act(t("zp")[:, a:a + ZW], pz[:, 0:ZW], F.Identity, ["pz" + s], ["zp%s%d" % (s, x) for x in range(2)], bank="pz" + s)
        for x, (lo, hi, rep) in enumerate(WALKS):
            n = 16 * (hi - lo + 1)
            while n < 16 * (hi - lo + 1) * rep:
                a = ZP[1] - n if x == 0 else ZP[1]
                b = a - n if x == 0 else a + n
                gcp(t("zp")[:, b:b + n], t("zp")[:, a:a + n], ["zp%s%d" % (s, x)], ["zp%s%d" % (s, x)])
                n *= 2

    def gath(r, h):
        s = str(h)
        t = lambda n: T[n + s]
        win, kw = t("tab")[:, 0:W], ["tab%sa" % s, "tab%sb" % s]
        fine = (r, h) in FINE
        dist = [(t("pd"), 256, "d0" + s, "pd" + s), (t("pz"), 384, "d1" + s, "pz" + s) if fine else (t("pd"), 384, "d0" + s, "pd" + s)]
        for ih, (d, a, key, bank) in enumerate(dist):
            for g in range(8):
                mm(d[:, a + 16 * g:a + 16 * g + 16], T.par[:, 128 * g:128 * g + 128], t("zt")[:], ["par%d" % g, "zt" + s], key, bank,
                   g == 0 and (fine or ih == 0))
        for x, (lo, hi, rep) in enumerate(WALKS):
            run, at = hi - lo + 1, 256 * (lo + x)
            col = lambda n, j, ih, w: t(n)[:, at + 128 * run * ih + 1 + j - lo:at + 128 * run * (ih + w):run]
            for ih, w in (((0, 1), (1, 1)) if x in SPLIT else ((0, 2),)):
                for j in range(lo, hi):
                    src = win.indirect(t("eu")[:, 16 * j + 8 * ih:16 * j + 8 * (ih + w)])
                    rd = kw + ["eu" + s + "ab"[j >= 4]]
                    wr = ["gg%s_%d_%d" % (s, j, c) for c in range(ih, ih + w)]
                    if j in ON_V:
                        ts(col("gg", j, ih, w), src, level(j), level(j), A.mult, A.add, rd, wr, ind=True)
                    else:
                        act(col("gg", j, ih, w), src, F.Identity, rd, wr, bias=level(j), scale=level(j), ind=True)
            for i in range(0, 16, rep):
                a, n = at + 16 * run * i, 16 * run * rep
                scan(t("mn")[:, a:a + n], t("gg")[:, a:a + n], t("zp")[:, ZP[x]:ZP[x] + n], A.max, A.min,
                     ["gg%s_%d_%d" % (s, j, i // 8) for j in range(lo, hi)] + ["zp%s%d" % (s, x), "gz%s%d" % (s, x)],
                     ["mn%s_%d_%d" % (s, x, c) for c in range(i, i + rep)])
            for ih, (d, a, key, bank) in enumerate(dist):
                for j in range(lo, hi):
                    out = d[:, a + j:a + 128:16]
                    mm(out, col("gg", j, ih, 1), T.wx[:, 16 - j:8 * RUN:RUN], ["wx", "gg%s_%d_%d" % (s, j, ih)], key, bank, False)
                    mm(out, col("mn", j, ih, 1), T.wm[:, 16 - j:8 * RUN:RUN], ["wm"] + ["mn%s_%d_%d" % (s, x, i) for i in range(8 * ih, 8 * ih + 8)],
                       key, bank, False)
        if fine:
            for ih, (d, a, key, bank) in enumerate(dist):
                act(t("mask")[:, 128 * ih:128 * ih + 128], d[:, a:a + 128], F.Sign, [key], ["mask%s%d" % (s, ih)], scale=-1.0, bank=bank)
        else:
            act(t("mask")[:], t("pd")[:, 256:512], F.Sign, ["d0" + s], ["mask%s%d" % (s, ih) for ih in range(2)], scale=-1.0, bank="pd" + s)

    def counts(r, h):
        s, rh = str(h), "%d%d" % (r, h)
        t = lambda n: T[n + s]
        si, pb, col = t("si"), t("pb"), t("col")
        pk = pb[:, 256:288]
        mm(pk, T.one[0:1, :], T.kp[0:1, :], ["one", "kp"], "pc" + s, "pb" + s, True)
        for ih in range(2):
            mm(pk, t("mask")[:, 128 * ih:128 * ih + 128], T.r2[:], ["r2a", "r2b", "mask%s%d" % (s, ih)], "pc" + s, "pb" + s, False)
        scan(si[:, 64:96], T.rst[:, 0:32], pk, A.mult, A.max, ["pc" + s, "rst"], ["key" + s], bank="pb" + s)
        ts(si[:, 96:98], si[:, 79:96:16], 15, None, A.bitwise_and, None, ["key" + s], ["na" + s])
        ts(t("offs")[:, 0:4:2], si[:, 96:98], -1.0, top, A.mult, A.add, ["na" + s, "top"], ["offs" + s])
        act(t("hot")[:, 0:1], si[:, 79:80], F.Sign, ["key" + s], ["hot" + s], bias=0.5 - 16 * 9)
        pa = pb[:, 300:301]
        mm(pa, T.blk2[:], t("hot")[:, 0:1], ["blk2", "hot" + s], "pA" + s, "pb" + s, True)
        mm(pa, T.one[0:1, :], T.iob[0:1, 16:17], ["one", "iob"], "pA" + s, "pb" + s, False)
        ts(field(r, h, 3), T.k32[:], pa, (1024.0 if r < RO - 1 else 96.0 * W) - SQ * SQ, A.mult, A.add, ["pA" + s, "k32"], ["sA" + rh], bank="pb" + s)
        if r < RO - 1:
            ts(col[:, 4:5], pa, lim, pa, A.is_lt, A.mult, ["pA" + s, "lim"], ["am" + s], bank="pb" + s)

    def best(r, h):
        s, rh = str(h), "%d%d" % (r, h)
        t = lambda n: T[n + s]
        si, sm, pr, offs = t("si"), t("sm"), t("pr"), t("offs")
        kw = ["tab%sa" % s, "tab%sb" % s]
        cut = lambda n: [n + s + "a", n + s + "b"]
        tt(sm[:, 80:96], t("w1")[:, 0:256].indirect(offs[:, 0:1]), sm[:, 16:32], A.mult, cut("w1") + ["offs" + s, "F" + s], ["qw" + s], ind=True)
        tt(si[:, 112:128], sm[:, 80:96], sm[:, 64:80], A.add, ["qw" + s, "c32" + s], ["ww" + s])
        ts(si[:, 128:144], si[:, 112:128], 5, W - 1, A.arith_shift_right, A.bitwise_and, ["ww" + s], ["ew" + s])
        cp(t("winu")[:], si[:, 128:144], ["ew" + s], ["winu" + s])
        act(t("xh")[:], t("tab")[:, 0:W].indirect(t("winu")[:, 0:16]), F.Identity, kw + ["winu" + s], ["xh" + s], scale=0.5, ind=True)
        act(field(r, h, 0), si[:, 128:144], F.Identity, ["ew" + s], ["sL" + rh], bias=-2048.0)
        act(sm[:, 96:112], t("e0")[:, 0:256].indirect(offs[:, 0:1]), F.Identity, cut("e0") + ["offs" + s], ["ek" + s], bias=-8192.0, ind=True)
        tt(field(r, h, 4, pair=True), T.hwl[:, 0:256].indirect(offs[:, 2:3]), sm[:, 96:112], A.add, ["hwl", "offs" + s, "ek" + s], ["sLo" + rh], ind=True)
        tt(field(r, h, 5, pair=True), T.hwh[:, 0:256].indirect(offs[:, 2:3]), sm[:, 96:112], A.add, ["hwh", "offs" + s, "ek" + s], ["sHi" + rh], ind=True)
        scan(t("ms")[:], T.rst[:], t("xh")[:], A.mult, A.max, ["rst", "xh" + s], ["ms" + s])
        mh = t("ms")[:, 15:256:16]
        cp(field(r, h, 1), mh, ["ms" + s], ["sM" + rh])
        exchange(r, h)
        yh = t("yh")[:, 16:32]
        tt(yh, mh, field(r, h, 2), A.add, ["ms" + s, "sQ" + rh], ["yh" + s])
        for c in range(2):
            mm(pr[:, 256 + 16 * c:272 + 16 * c], T.pick[:, 128 * c:128 * c + 128], yh, ["pick", "yh" + s], "py%d%s" % (c, s), "pr" + s, True)
        act(t("yb")[:], pr[:, 256:288], F.Identity, ["py0" + s, "py1" + s], ["yb" + s], bias=-YOFF, bank="pr" + s)
        for l in range(16):
            mm(pr[:, 288:290], T.uw[:, 15 - l:143 - l], t("yb")[:, l:32:16], ["uw", "yb" + s], "pt" + s, "pr" + s, l == 0)
        act(si[:, 144:146], pr[:, 288:290], F.Identity, ["pt" + s], ["pli" + s], bank="pr" + s)
        ts(si[:, 146:148], si[:, 144:146], 127, None, A.bitwise_and, None, ["pli" + s], ["plj" + s])
        for c in range(2):
            act(t("plu")[:, c:c + 1], si[:, 146 + c:147 + c], F.Identity, ["plj" + s, "lbase%d" % c], ["plu%d%s" % (c, s)], bias=cf[:, 17 + c:18 + c])
        cp(t("tab")[:, 0:W].indirect(t("plu")[:, 0:2]), t("yb")[:], ["plu0" + s, "plu1" + s, "yb" + s], kw, c=180.0)
        if r == RO - 1:
            dma("Y", T.yx[64 * h:64 * h + 64, :], t("tab")[0:64, :], kw + ["s" + rh], ["yx" + s], "d_yx" + s, LAT_DMA + 1800)

    def leave(h):
        s = str(h)
        t = lambda n: T[n + s]
        si, zl, pr, pb = t("si"), t("zl"), t("pr"), t("pb")
        arrive(RO - 1, h)
        act(t("zt")[:], field(RO - 1, h, 3, True), F.Identity, ["rcv%d%d" % (RO - 1, h)], ["zt" + s])
        ka = unfold(pb, T.pick, 128, t("zt"), 16, ["pick", "zt" + s], "oa" + s, "pb" + s)
        tt(si[0:64, 64:96], si[0:64, 152:184], pb[0:64, 0:32], A.add, ["sq" + s] + ka, ["key" + s], bank="pb" + s)
        ts(si[0:64, 112:144], si[0:64, 64:96], 5, W - 1, A.arith_shift_right, A.bitwise_and, ["key" + s], ["ww" + s, "ew" + s])
        cp(t("of")[0:64, 32:64], si[0:64, 112:144], ["ww" + s], ["oc" + s])
        ko = unfold(pr, T.pick, 128, zl, 32, ["pick", "zl" + s, "z" + s], "ol" + s, "pr" + s)
        act(t("of")[0:64, 0:32], pr[0:64, 0:32], F.Identity, ko, ["ol" + s], bias=2048.0, bank="pr" + s)
        act(t("oz")[0:64, :], pr[0:64, 32:64], F.Identity, ko, ["oz" + s], bank="pr" + s)
        dma("S", T.yz[64 * h:64 * h + 64, :], t("oz")[0:64, :], ["oz" + s], ["yz" + s], "d_yz" + s, LAT_DMA)
        dma("Y", T.ya[4 * h:4 * h + 4, :], t("of")[0:64:16, 32:64], ["oc" + s], ["ya" + s], "d_ya" + s, LAT_DMA)
        dma("Y", T.yl[64 * h:64 * h + 64, :], t("of")[0:64, 0:32], ["ol" + s], ["yl" + s], "d_yl" + s, LAT_DMA)

    for r in range(RO):
        for h in range(2):
            prep(r, h)
            gath(r, h)
            counts(r, h)
            best(r, h)
    leave(0)
    leave(1)
    return ops, groups


def plan(ops):
    n = len(ops)
    nil = 0.0 * CV
    cases = []
    for c in range(len(CV)):
        lat = [float((o["lat"] + nil)[c]) for o in ops]
        pred = [[(d, lat[d] if ops[d]["sem"] is not None else float(LAT_X[c]) if ops[d]["eng"] != o["eng"]
                  else 0.0 if o["eng"] == "P" else float(LAT_SAME[c])) for d in sorted(o["deps"])]
                + ([(o["after"], 0.0)] if "after" in o else []) for o in ops]
        succ = [[] for _ in ops]
        for k in range(n):
            for d, gap in pred[k]:
                succ[d].append((k, gap))
        cases.append(([float((o["cost"] + nil)[c]) for o in ops], lat, pred, succ))

    def replay(order, case):
        cost, lat, pred, _ = case
        free, st = {e: 0.0 for e in "VSPGYZ"}, [0.0] * n
        for k in order:
            st[k] = max([st[j] + cost[j] + gap for j, gap in pred[k]] + [free[ops[k]["eng"]]])
            free[ops[k]["eng"]] = st[k] + cost[k]
        return max(st[k] + cost[k] + lat[k] for k in range(n)), st

    def place(seq, back, cost, slack, case):
        _, lat, pred, succ = case
        busy = {e: [] for e in "VSPGYZ"}
        st = [0.0] * n
        for k in seq:
            c = cost[k]
            t = max([st[j] + cost[j] + gap * slack for j, gap in (succ[k] if back else pred[k])] + [lat[k] if back else 0.0])
            line = busy[ops[k]["eng"]]
            lo, hi = 0, len(line)
            while lo < hi:
                m = (lo + hi) // 2
                if line[m][1] <= t:
                    lo = m + 1
                else:
                    hi = m
            while lo < len(line) and line[lo][0] < t + c:
                t = max(t, line[lo][1])
                lo += 1
            line.insert(lo, (t, t + c))
            st[k] = t
        return st

    best, rng = None, np.random.default_rng(7)
    for j in range(TRIES):
        case = cases[j % len(cases)]
        cost = [c * (0.85 + 0.3 * float(rng.random())) for c in case[0]]
        slack = 0.8 + 0.8 * float(rng.random())
        seq = list(range(n)) if j < FRESH else best[1]
        for _ in range(PASSES):
            st = place(seq, False, cost, slack, case)
            order = sorted(range(n), key=lambda k: (st[k], k))
            ends = [replay(order, c)[0] for c in cases]
            if best is None or sum(ends) < sum(best[0]):
                best = (ends, order)
            bk = place(sorted(range(n), key=lambda k: (-st[k] - cost[k], -k)), True, cost, slack, case)
            seq = sorted(range(n), key=lambda k: (-bk[k] - cost[k], k))
    return best[1], replay(best[1], cases[0])[1], best[0], cases[0][0]


def rank_program(g, core, T, topo):
    rank = T.rank_of(core)
    if rank is None:
        return
    ops, groups = build(T, topo, rank)
    if "order" not in PLAN:
        PLAN["order"] = plan(ops)[0]
    order = PLAN["order"]
    at = {k: j for j, k in enumerate(order)}
    last = set(max(gr, key=lambda k: at[k]) for gr in groups)
    queue = {"V": g.vector, "S": g.scalar, "P": g.tensor, "G": g, "Y": g.sync}
    order = [k for k in order if ops[k]["fn"] is not None]
    known = {e: {} for e in queue}
    snap, waits, marked = {}, {}, set()
    for k in order:
        o = ops[k]
        kn = known[o["eng"]]
        ws = []
        for d in sorted(o["deps"], key=lambda d: -at[d]):
            p = ops[d]
            if p["sem"] is None and p["eng"] == "P" and o["eng"] == "P":
                continue
            key = p["sem"][0] if p["sem"] is not None else p["eng"]
            if kn.get(key, -1) >= at[d]:
                continue
            ws.append(d)
            if p["sem"] is None:
                marked.add(d)
            kn[key] = at[d]
            if p["sem"] is None or p["sem"][0].startswith("d_"):
                for x, v in snap[d].items():
                    if kn.get(x, -1) < v:
                        kn[x] = v
        waits[k] = ws
        snap[k] = dict(kn)
    count, tick = {e: 0 for e in queue}, {}
    for k in order:
        o = ops[k]
        e = o["eng"]
        q = queue[e]
        for d in waits[k]:
            p = ops[d]
            if p["sem"] is not None:
                q.wait_ge(T.sem[p["sem"][0]], p["sem"][1])
            else:
                q.wait_ge(T.sem["e" + p["eng"]], tick[d])
        ins = o["fn"](q, k in last) if e == "P" else o["fn"](q)
        if o["sem"] is not None:
            if o["sem"][0].startswith("d_"):
                ins.then_inc(T.sem[o["sem"][0]], 16)
        elif k in marked:
            count[e] += 1
            tick[k] = count[e]
            ins.then_inc(T.sem["e" + e], 1)
    for n in ("yx", "yl", "yz", "ya"):
        for h in range(2):
            g.sync.wait_ge(T.sem["d_%s%d" % (n, h)], 16)
    for r in range(RO):
        for h in range(2):
            g.wait_ge(T.sem["s%d%d" % (r, h)], len(HOPS))
